import numpy as np, ml_dtypes
CORES = [66,74,82,90,194,202,210,218]
N = 8
BF = ml_dtypes.bfloat16
def gentries(a):
    return np.ascontiguousarray(a.reshape(8, 16, -1).transpose(0, 2, 1)).reshape(8, -1)
def gtable(e):
    e = np.asarray(e); return np.ascontiguousarray(e.reshape(8, -1, 16).transpose(0, 2, 1)).reshape(128, -1).astype(np.int32)
E, G, M, S, R = 1024, 128, 192, 2, 4
V, W = S * M, E + (N - 1) * G
def pick(rng, shape, lo, hi):
    return np.where(rng.random(shape) < 0.5, lo, hi)
def parts(rng):
    a = np.minimum((16 * (0.25 + 0.75 * rng.random((N, 8, 1, E))) * rng.random((N, 8, 16, E))).astype(np.int64), 15)
    hot = rng.integers(0, W, (N, 8, 128)); hot[..., :64] = rng.integers(0, V, (N, 8, 64))
    h = np.take_along_axis(hot, rng.integers(0, 128, (N, 8, V * 16)), 2).reshape(N, 8, V, 16)
    return {"a": a, "k": rng.integers(0, 8, (N, 8, 16, 2048)), "be": np.exp2(-10 + 3 * rng.random((N, 8, 16))),
            "ti": rng.integers(0, 1024, (N, 8, E)), "kd": rng.integers(0, 8, (N, 8, E)), "cl": rng.integers(0, 16, (N, 8, V)), "bg": rng.integers(0, 4096, (N, 8, V)), "us": rng.integers(0, 256, (N, 8, R * M)),
            "lp": np.where(rng.random((N, 8, E)) < 0.25, -1, rng.integers(0, W, (N, 8, E))),
            "ca": np.where(rng.random((N, 8, V, 16)) < 0.4, h, rng.integers(0, W, (N, 8, V, 16))),
            "snd": np.ascontiguousarray(np.argsort(rng.random((N, 8, N - 1, E)), axis=-1)[..., :G])}
def pack(p):
    d = {"a0": p["a"].reshape(N, 128, E).astype(np.float32).astype(BF), "k0": p["k"].reshape(N, 128, 2048).astype(np.float32).astype(BF), "be": p["be"].reshape(N, 128, 1).astype(np.float32)}
    for k in ("ti", "kd", "cl", "bg", "us", "lp"): d[k] = p[k].astype(np.int32)
    d["ca"] = np.stack([gtable(x.reshape(8, -1)) for x in p["ca"]]); d["snd"] = np.stack([gtable(x.reshape(8, -1)) for x in p["snd"]])
    return d
def setup_inputs(rng):
    return pack(parts(rng))
def setup_inputs_spread(rng):
    p = parts(rng)
    p["a"] = np.minimum((16 * np.exp2(-3 * rng.random((N, 8, 1, E))) * rng.random((N, 8, 16, E))).astype(np.int64), 15)
    p["k"] = np.minimum((8 * np.exp2(-2 * rng.random((N, 8, 1, 2048))) * rng.random((N, 8, 16, 2048))).astype(np.int64), 7)
    for k, n, e in (("ti", 1024, 3.0), ("bg", 4096, 4.0), ("us", 256, 0.5), ("cl", 16, 2.0), ("ca", W, 2.0)):
        p[k] = np.minimum((n * rng.random(p[k].shape) ** e).astype(np.int64), n - 1)
    p["lp"] = np.where(rng.random((N, 8, E)) < 0.5, -1, rng.integers(0, W, (N, 8, E)))
    r = int(rng.integers(0, N)); p["be"][r] = 2.0 ** -7
    p["ti"][r, :, :V] = rng.integers(0, 48, (8, V)); p["ti"][r, :, V:] = rng.integers(976, 1024, (8, E - V))
    tw = ghosts(p["ti"][:, :, None], p["snd"])[r, :, 0]
    for g in range(8):
        far = np.flatnonzero(tw[g] >= 976)
        p["ca"][r, g] = rng.choice(far, (V, 16)); p["lp"][r, g] = np.where(p["lp"][r, g] < 0, -1, rng.choice(far, E))
    return pack(p)
def setup_inputs_ends(rng):
    p = parts(rng)
    s = rng.random((N, 8, 1, E)); p["a"] = np.where(s < 0.25, 0, np.where(s < 0.5, 15, pick(rng, (N, 8, 16, E), 0, 15)))
    s = rng.random((N, 8, 1, 2048)); p["k"] = np.where(s < 0.25, 0, np.where(s < 0.5, 7, pick(rng, (N, 8, 16, 2048), 0, 7)))
    p["a"][:, ::2, :, 0] = 15; p["a"][..., 2] = 0; p["a"][..., E - 1] = 15
    for j in (0, 63, 1984, 2047): p["k"][..., j] = 7
    p["k"][..., 1991] = 0
    p["be"] = pick(rng, (N, 8, 16), 2.0 ** -10, 2.0 ** -7)
    for k, lo, hi in (("ti", 0, 1023), ("kd", 0, 7), ("us", 0, 255), ("lp", -1, W - 1)):
        p[k] = np.where(rng.random(p[k].shape) < 0.8, pick(rng, p[k].shape, lo, hi), p[k])
    p["cl"] = pick(rng, (N, 8, V), 0, 15); p["bg"] = pick(rng, (N, 8, V), 0, 4095)
    for j in (0, V - 1, E - 1): p["kd"][..., j] = 7
    p["ti"][..., 0] = 1023; p["ti"][..., V - 1] = 0; p["ti"][..., E - 1] = 1023
    p["bg"][..., V - 1] = 4095 * ((np.arange(N)[:, None] + np.arange(8)[None, :]) % 2)
    at = (rng.random((N, 8, V, 1)) < 0.45) | (rng.random((N, 8, V, 16)) < 0.4)
    p["ca"] = np.where(at, pick(rng, (N, 8, V, 16), 0, W - 1), rng.integers(0, W, (N, 8, V, 16)))
    p["ca"][:, :, 0] = W - 1; p["ca"][:, :, V - 1] = W - 1; p["ca"][:, :, 1] = 2
    both = np.concatenate([np.arange(G // 2), np.arange(E - (G - G // 2), E)])
    s = both[np.argsort(rng.random((N, 8, N - 1, G)), axis=-1)]; j = np.argmax(s == E - 1, axis=-1)[..., None]
    np.put_along_axis(s, j, s[..., -1:].copy(), -1); s[..., -1] = E - 1
    p["snd"] = s
    return pack(p)
def setup_inputs_corners(rng):
    p = parts(rng)
    for r in range(N):
        for g in range(8):
            x = (g + r) % 8
            for k, cap, n, kind in (("a", 15, E, x % 4), ("k", 7, 2048, (x // 2) % 4)):
                if kind == 0: p[k][r, g] = cap - rng.integers(0, 2, (16, n))
                elif kind == 1: p[k][r, g] = rng.integers(0, 2, (16, n))
                elif kind == 2: p[k][r, g] = np.broadcast_to(pick(rng, (1, n), 0, cap), (16, n))
    e = np.broadcast_to(np.arange(E), (N, 8, E)); o = rng.integers(0, 8, (N, 8, E))
    p["lp"] = np.choose(o, [np.full_like(e, -1), e, (e + 1) % E, np.zeros_like(e), np.full_like(e, E - 1), np.full_like(e, E), np.full_like(e, W - 1), p["lp"]])
    v = np.broadcast_to(np.arange(V)[:, None], (N, 8, V, 16)); o = rng.integers(0, 10, (N, 8, V, 16))
    for i, c in enumerate((0, V - 1, E - 1, E, W - 1)): p["ca"] = np.where(o == i, c, p["ca"])
    p["ca"] = np.where(o == 5, v, p["ca"])
    p["us"] = rng.choice(np.array([0, 1, 127, 128, 254, 255]), (N, 8, R * M)); p["bg"] = rng.choice(np.array([0, 0, 0, 1, 4094, 4095]), (N, 8, V))
    return pack(p)
def setup_inputs_crowd(rng):
    p = parts(rng); h = int(rng.integers(0, N)); x = rng.integers(V, E, 8); x[0] = E - 1; x[1] -= x[1] % 2; x[3] = 0
    tv = rng.integers(100, 900, 8); kv = rng.integers(0, 8, 8); cv = rng.integers(0, 16, 8)
    for g in range(8):
        p["a"][h, g, :, x[g]] = np.maximum(p["a"][h, g, :, x[g]], 1); p["a"][h, g, cv[g], x[g]] = 1
        for d in range(1, N):
            row = p["snd"][h, g, d - 1]; j = np.flatnonzero(row == x[g])
            if j.size: row[j[0]] = row[G - 1]
            row[G - 1] = x[g]
    for r in range(N):
        for g in range(8):
            w = g if r == h else (g - 1) % 8
            if w == 7: continue
            c = int(x[w]) if r == h else E + ((r - h) % N - 1) * G + G - 1
            p["ti"][r, g, :V] = tv[w]; p["kd"][r, g, :V] = kv[w]; p["bg"][r, g] = 0; p["k"][r, g] = np.maximum(p["k"][r, g], 1)
            if w % 2 == 0: p["cl"][r, g] = cv[w]
            if w == 6: p["ca"][r, g] = rng.choice(np.array([0, c, E, W - 1]), (V, 16)); continue
            p["ca"][r, g] = c
            if w >= 3:
                for s in range(S):
                    i = (0, M - 1, int(rng.integers(0, M)))[w - 3]; p["ca"][r, g, s * M + i] = rng.integers(0, W, 16)
    for g in range(7):
        if x[g] >= V: p["ti"][h, g, x[g]] = tv[g] + rng.integers(0, 65)
    p["cl"][h, 1, ::M] = cv[1]
    q = (h + 1) % N; i = np.arange(M); n = min(G, M); ev = p["snd"][h, 7, 0, :n]; o = V + i[n:]
    tc = 400 + 32 * (i >> 6) + rng.integers(0, 32, M); kc = (i >> 3) % 8
    p["ti"][q, 0, :V] = 400; p["kd"][q, 0, :V] = np.tile(i % 8, S); p["bg"][q, 0] = 0; p["k"][q, 0] = rng.integers(1, 3, (16, 2048))
    p["ca"][q, 0] = np.tile(np.where(i < n, E + i, V + i), S)[:, None]; p["lp"][q, 0, o] = -1
    for b, g, c, lo, hi in ((h, 7, ev, 0, n), (q, 0, o, n, M)):
        p["a"][b, g][:, c] = rng.integers(1, 3, (16, hi - lo)); p["ti"][b, g, c] = tc[lo:hi]; p["kd"][b, g, c] = kc[lo:hi]
    return pack(p)
def setup_inputs_calm(rng):
    p = parts(rng)
    for r in range(N):
        for g in range(8):
            kind = (g + r) % 4
            if kind == 0: p["a"][r, g] = (np.arange(16)[:, None] == rng.integers(0, 16, (1, E))) & (rng.random((1, E)) < 0.5)
            elif kind == 3: p["a"][r, g] = rng.integers(0, 4, (16, E))
            else: p["a"][r, g] = kind
            p["k"][r, g] = (1, 1, 0, 3)[kind]
            if kind == 2: p["k"][r, g] = rng.integers(0, 3, (16, 2048))
    p["ca"] = rng.integers(0, W, (N, 8, V, 16)); p["us"] = 16 * rng.integers(0, 16, (N, 8, R * M)); p["bg"] = rng.choice(np.array([0, 0, 0, 1, 16, 256]), (N, 8, V))
    r = int(rng.integers(0, N)); p["k"][r, (1 - r) % 4] = 0
    g = 4 + (2 - r) % 4; p["us"][r, g] = 255; p["bg"][r, g] = 4095
    return pack(p)
def check_ranges(d):
    bad = []
    for k, lo, hi in (("a0", 0, 15), ("k0", 0, 7), ("be", 2.0 ** -10, 2.0 ** -7), ("ti", 0, 1023), ("kd", 0, 7), ("cl", 0, 15), ("bg", 0, 4095), ("us", 0, 255), ("lp", -1, W - 1), ("ca", 0, W - 1), ("snd", 0, E - 1)):
        v = np.asarray(d[k]).astype(np.float64)
        if not np.all((v >= lo) & (v <= hi)): bad.append("range of " + k)
        elif k in ("a0", "k0") and np.any(v != np.floor(v)): bad.append("whole numbers of " + k)
    s = np.sort(np.stack([gentries(x) for x in np.asarray(d["snd"])]).reshape(N, 8, N - 1, G), axis=-1)
    if np.any(s[..., 1:] == s[..., :-1]): bad.append("repeated event in a block of snd")
    return bad
def ghosts(x, sl):
    out = []
    for r in range(N):
        w = [x[r]]
        for d in range(1, N):
            q = (r - d) % N
            w.append(np.roll(np.take_along_axis(x[q], sl[q, :, d - 1][:, None, :], 2), 1, axis=0))
        out.append(np.concatenate(w, axis=2))
    return np.stack(out)
def reference(a0, k0, be, ti, kd, cl, bg, us, lp, ca, snd):
    A = a0.astype(np.float32).astype(np.int64).reshape(N, 8, 16, E); K = k0.astype(np.float32).astype(np.int64).reshape(N, 8, 16, 2048)
    beta = be.astype(np.float64).reshape(N, 8, 16, 1); T, D, cls, B, U, L = [v.astype(np.int64) for v in (ti, kd, cl, bg, us, lp)]
    C = np.stack([gentries(x) for x in ca]).astype(np.int64); sl = np.stack([gentries(x) for x in snd]).astype(np.int64).reshape(N, 8, N - 1, G)
    TW = ghosts(T[:, :, None], sl)[:, :, 0]; DW = ghosts(D[:, :, None], sl)[:, :, 0]
    lam = []
    for t in range(R):
        lo = (t % S) * M; AW = ghosts(A, sl)
        c = C[:, :, 16 * lo:16 * (lo + M)]
        lag = np.abs(np.repeat(T[:, :, lo:lo + M], 16, axis=2) - np.take_along_axis(TW, c, 2))
        bn = 64 * (lag >> 5) + 8 * np.repeat(D[:, :, lo:lo + M], 16, axis=2) + np.take_along_axis(DW, c, 2)
        pr = np.take_along_axis(AW, c[:, :, None], 3) * np.take_along_axis(K, bn[:, :, None], 3)
        lam.append(np.add.reduce((np.exp(-beta * lag[:, :, None]) * pr).reshape(N, 8, 16, M, 16), axis=4))
        w = np.add.reduce(pr, axis=2).reshape(N, 8, M, 16); cum = np.add.accumulate(w, axis=3)
        hit = 256 * cum > (U[:, :, t * M:(t + 1) * M] * (B[:, :, lo:lo + M] + cum[..., 15]))[..., None]
        el = np.any(hit, axis=3); first = np.argmax(hit, axis=3)[..., None]
        cc = c.reshape(N, 8, M, 16); par = np.take_along_axis(cc, first, 3)[..., 0]; pb = np.take_along_axis(bn.reshape(N, 8, M, 16), first, 3)[..., 0]
        add = np.zeros_like(A)
        for r in range(N):
            for g in range(8):
                i = np.flatnonzero(el[r, g]); cg = cls[r, g, lo:lo + M]
                col, j = np.unique(par[r, g, i], return_index=True); z = cg[i[j]]; own = col < E
                np.add.at(add, (r, g, z[own], col[own]), 1)
                y = col[~own] - E; d = y // G + 1; q = (r - d) % N; h = (g - 1) % 8
                np.add.at(add, (q, h, z[~own], sl[q, h, d - 1, y % G]), 1)
                if t < R - 1:
                    b, j = np.unique(pb[r, g, i], return_index=True); z = cg[i[j]]
                    K[r, g, z, b] = np.minimum(K[r, g, z, b] + 1, 7)
        A = np.minimum(A + add, 15)
        if t < R - S:
            L[:, :, lo:lo + M] = np.where(el, par, L[:, :, lo:lo + M])
            up = np.where(el & (par < E), np.take_along_axis(L, np.minimum(par, E - 1), 2), -1)[..., None]
            least = np.argmin(w, axis=3)[..., None]
            C[:, :, 16 * lo:16 * (lo + M)] = np.where((np.arange(16) == least) & (up >= 0), up, cc).reshape(N, 8, 16 * M)
    return {"yl": np.concatenate(lam, axis=3).reshape(N, 128, R * M).astype(np.float32), "ya": A.reshape(N, 128, E).astype(np.float32)}

def check_inputs(d):
    bad = list(check_ranges(d))
    if not bad:
        for name, y in reference(**d).items():
            for q in range(N):
                v = np.abs(np.asarray(y[q], np.float64)); s = np.sqrt(np.mean(v * v))
                if v.max() > 9 * s or s < 2.0 ** -6: bad.append('%s of rank %d is uneven or too small' % (name, q))
    return bad

@@ -1,0 +1,706 @@
+import math
+from concourse.bass import DstId, RemoteDMATransfer
+from concourse.mybir import AluOpType as OP, ActivationFunctionType as AF
+
+N, E, G, M, R = 8, 1024, 128, 192, 4
+W = E + (N - 1) * G
+GW = (N - 1) * G
+C = 16 * M
+RW = 2144
+PL = 4 * RW
+ZW = PL + 7 * E
+KWID = 16 + 2048 + M
+BF, F32, F16, I32, U16 = "bfloat16", "float32", "float16", "int32", "uint16"
+
+SCRATCH = {}
+for _n, _w, _d in (
+        ("zb", ZW, BF), ("aw", R * W, BF), ("ash", E, BF), ("tks", E, BF), ("tkw", W, BF), ("fb", 5 * GW, BF),
+        ("rv", R * GW, BF), ("kw", KWID, BF), ("kg", C, BF), ("tg", C, BF), ("ag", 2048, BF), ("pr", R * C, BF), ("rg", 2 * C, F32),
+        ("so", 2048, F32), ("rt", 2048, F32), ("lw", E + 16, F32), ("yaf", E, F32), ("ylf", R * M, F32),
+        ("e15", R * M, F32), ("t64", 512, I32), ("h64", 256, F16), ("dg", 128, BF), ("sni", 56, I32),
+        ("snu", 56, U16), ("cai", 2 * M, I32), ("cu", 2 * M, U16), ("c1", 2 * M, F16), ("m8", 384, I32),
+        ("m8h", 384, F16), ("mb", 384, I32), ("mbf", 384, F32), ("ex", 8 * 128, BF), ("ex32", 128, F32),
+        ("exv", 128, BF), ("bet", 8, F32), ("urep", R * M, F32), ("oh", 2 * M, BF), ("ji", 256, I32),
+        ("pci", 8, I32), ("pcf", 8, F32), ("mk8", 16, F32), ("mc", 128, BF), ("cm", 13 * 128, BF),
+        ("sel", 16 * 128, BF), ("r16", M, F32), ("thr", 2 * M, F32), ("rst", M, BF), ("big", M, F32),
+        ("wc", 64, F32), ("dum", 80, F32), ("w16", 2 * M, F16), ("th", M, F32), ("hd", 2 * M, F16),
+        ("rep", 3 * M, F16), ("lst", 48, F32), ("zz", 12 * M, BF), ("fl", 2 * M, BF), ("sm", 48, F32),
+        ("offs", 64, U16), ("kt", M, BF), ("oh7", 2 * M, BF), ("bi", 4 * M, I32), ("bf", 5 * M, F32), ("b1", R * M, F16),
+        ("l16", M, F16), ("binu", R * M, U16), ("xi", 2 * M, I32), ("up", M, F16), ("dlt", R * M, U16), ("rec", M, BF), ("ty", 4 * 232, F32),
+        ("hi", 4 * 64, F32)):
+    SCRATCH[_n] = ("sbuf", [128, _w], _d)
+for _b in range(8):
+    SCRATCH["p%d" % _b] = ("psum", [128, 512], F32)
+NDMA = 40
+SEMAPHORES = ["cv", "cs", "ct", "cg", "sent"] + ["arr%d" % _i for _i in range(13)] + ["dm%d" % _i for _i in range(NDMA)]
+
+CY, PE, TX, HOP, PASSES = 0.00104, 0.00055, 4.5, 0.1, 2
+CASES = ((0.8, 0.67, 0.42, 0.7), (1.0, 1.0, 1.0, 1.0), (1.0, 1.0, 1.0, 1.5), (1.2, 1.33, 1.58, 1.3))
+ORDER = {}
+LW = 256
+URGE = {'ga': 30, 'skg00': 8, 'skg10': 9, 'skg20': 7, 'skg01': 6, 'skg11': 6, 'skg21': 6, 'vlst20': 1, 'srt00': 8, 'gcma0': -1,
+        'vb100': -1, 'vp310': 1, 'vrec00': -2, 'stg02': -1, 'srg22': 8, 'vrep00': -1, 'gtya0': 30, 'vpr20': 1,
+        'voffs30': 1, 'gr16a0': 4, 'vxia0': -4, 'vbinua0': 30, 'vzz20': 2, 'vlw00': 4, 'vash10': 4, 'vzz10': -10,
+        'vpr11': -1, 'vpr30': -1, 'skga2': -10, 'vsm20': 1, 'gwca0': 15, 'skg12': -4}
+NI, NSH, NUSH, E0, E1, U0, U1, ONES, TRI, DM, DU, DL, R15 = range(13)
+XU0, XU1, XC, XT, XK, XL0, XL1, XL2 = range(8)
+
+
+def arrange(ops, pre):
+    n = len(ops)
+    after = [[] for _ in range(n)]
+    for i in range(n):
+        for j in pre[i]:
+            after[j].append(i)
+    tail = [0.0] * n
+    for i in range(n - 1, -1, -1):
+        tail[i] = ops[i]["c"] + ops[i]["l"] + max([tail[j] + HOP for j in after[i]] + [0.0])
+
+    def place(seq, back):
+        start, busy = [0.0] * n, {}
+        for i in seq:
+            o, s = ops[i], 0.0
+            for j in (after[i] if back else pre[i]):
+                hop = 0.0 if (o["q"] == "t" and ops[j]["q"] == "t") else HOP
+                s = max(s, start[j] + ops[j]["c"] + (o["l"] if back else ops[j]["l"]) + hop)
+            if back and not after[i]:
+                s = o["l"]
+            if o["q"] != "x":
+                row, k = busy.setdefault(o["q"], []), 0
+                while k < len(row) and row[k][0] < s + o["c"] - 1e-9:
+                    s = max(s, row[k][1])
+                    k += 1
+                row.insert(k, (s, s + o["c"]))
+            start[i] = s
+        return start
+
+    def length(order, f, ga, sc, tx):
+        done, free = [0.0] * n, {}
+        for i in order:
+            o = ops[i]
+            s = free.get(o["q"], 0.0) if o["q"] != "x" else 0.0
+            for j in pre[i]:
+                s = max(s, done[j] + (0.0 if (o["q"] == "t" and ops[j]["q"] == "t") else HOP))
+            free[o["q"]] = s + o["c"] * f * (ga if o["m"] == "ga" else sc if o["m"] == "sc" else 1.0)
+            done[i] = free[o["q"]] + o["l"] * (tx if o["k"] == "x" else 1.0)
+        return max(done)
+
+    def ranked(worth):
+        w = [worth[i] + URGE.get(ops[i]["tag"], 0.0) for i in range(n)]
+        for i in range(n - 1, -1, -1):
+            w[i] = max([w[i]] + [w[j] + 1e-6 for j in after[i]])
+        return sorted(range(n), key=lambda i: (-w[i], i))
+
+    seq, best = ranked(tail), None
+    for _ in range(PASSES):
+        start = place(seq, False)
+        order = sorted(range(n), key=lambda i: (start[i], i))
+        end = sum(length(order, *m) / (m[0] * (m[1] + m[2] + 2)) for m in CASES)
+        if best is None or end < best[0]:
+            best = (end, order)
+        late = place(sorted(range(n), key=lambda i: (-start[i] - ops[i]["c"] - ops[i]["l"], -i)), True)
+        seq = ranked([late[i] + ops[i]["c"] for i in range(n)])
+    ORDER["end"] = best[0]
+    return best[1]
+
+
+def emit(g, T, ops):
+    queues = {"v": g.vector, "s": g.scalar, "t": g.tensor, "g": g, "y": g.sync}
+    log, bank, pre = {}, {}, []
+    for i, o in enumerate(ops):
+        d = set()
+        for acc, wr in ((o["r"], False), (o["w"], True)):
+            for (n, a, b) in acc:
+                for (a2, b2, j, w2) in log.get(n, ()):
+                    if a < b2 and a2 < b and (wr or w2):
+                        d.add(j)
+        for n in set(x[0] for x in o["r"] + o["w"]):
+            if SCRATCH[n][0] == "psum":
+                run = bank.setdefault(n, [o["q"], [], []])
+                if run[0] != o["q"]:
+                    run[0], run[1], run[2] = o["q"], [], run[1]
+                d.update(run[2])
+                if o["q"] == "t":
+                    d.update(run[1][-1:])
+                run[1].append(i)
+        if o["k"] == "x":
+            d.add(i - 1)
+        d.update(o.get("after", ()))
+        pre.append(d)
+        for (n, a, b) in o["w"]:
+            log[n] = [x for x in log.get(n, []) if not (a <= x[0] and x[1] <= b)] + [(a, b, i, True)]
+        for (n, a, b) in o["r"]:
+            log.setdefault(n, []).append((a, b, i, False))
+    key = (len(ops), CY, PE, TX, HOP, PASSES)
+    if key not in ORDER:
+        ORDER[key] = arrange(ops, pre)
+    order = ORDER[key]
+    place = dict((i, p) for p, i in enumerate(order))
+    deps = {}
+    for i in order:
+        o, best, keep = ops[i], {}, []
+        for j in pre[i]:
+            if o["k"] == "x" or j in o.get("after", ()) or (o["q"] == "t" and ops[j]["q"] == "t"):
+                continue
+            if ops[j]["k"] == "c":
+                q = ops[j]["q"]
+                if q not in best or place[j] > place[best[q]]:
+                    best[q] = j
+            else:
+                assert ops[j]["k"] != "r"
+                keep.append(j)
+        deps[i] = sorted(keep + list(best.values()))
+    needed = set(j for d in deps.values() for j in d)
+    mark, total, waited, nd = {}, {}, {}, [0]
+    for i in order:
+        o = ops[i]
+        if o["k"] == "x":
+            mark[i] = (o["sem"], o["n"])
+            total[o["sem"]] = o["n"]
+            continue
+        q = queues[o["q"]]
+        for j in deps[i]:
+            s, n = mark[j]
+            if waited.get((o["q"], s), 0) < n:
+                q.wait_ge(T.sem[s], n)
+                waited[(o["q"], s)] = n
+        ins = o["f"](q)
+        if o["k"] == "d":
+            s = "dm%d" % nd[0]
+            nd[0] += 1
+            ins.then_inc(T.sem[s], 16)
+            mark[i] = (s, 16)
+            total[s] = 16
+        elif o["k"] == "r":
+            total["sent"] = total.get("sent", 0) + o["n"]
+        elif i in needed:
+            s = "c" + o["q"]
+            total[s] = total.get(s, 0) + 1
+            ins.then_inc(T.sem[s], 1)
+            mark[i] = (s, total[s])
+    for s, n in total.items():
+        if waited.get(("g", s), 0) < n:
+            g.wait_ge(T.sem[s], n)
+
+
+def rank_program(g, core, T, topo):
+    rank = T.rank_of(core)
+    if rank is None:
+        return
+    ops, sends, tag = [], [], ["a"]
+
+    def v(n, a=None, b=None, st=1, p=None):
+        if a is None:
+            a, b = 0, SCRATCH[n][1][1]
+        ps = slice(0, 128) if p is None else slice(p[0], p[1])
+        last = a + ((b - a - 1) // st) * st + 1
+        ap = T[n][ps, a:b] if st == 1 else T[n][ps, a:last:st]
+        return (ap, [(n, a, last)], (b - a - 1) // st + 1)
+
+    def ind(w, o):
+        return (w[0].indirect(o[0]), w[1] + o[1], 16 * o[2], w[1], o[1])
+
+    def span(q, k, outs, ins, two):
+        full = [x for x in outs + ins if isinstance(x, tuple)]
+        wide = [SCRATCH[x[1][0][0]][2] in (F32, I32) for x in full if x[2] == full[0][2]]
+        if k == "x":
+            return 0.0, TX
+        if k == "r":
+            return 0.5, 0.0
+        if k == "d":
+            return 0.1, 2.0 + full[0][2] * (4 if wide[0] else 2) * 128 / 500e3
+        n = outs[0][2]
+        if q == "t":
+            return max(64, n) * PE * (4 if SCRATCH[ins[1][1][0][0]][2] == F32 else 1), 0.0
+        if q == "g":
+            return 0.2 + 2 * n * CY, 0.0
+        if len(outs[0]) == 5:
+            return 0.06 + 3.8 * n * CY, 0.0
+        if len(ins[0]) == 5:
+            return 0.07 + 1.56 * n * CY, 0.0
+        if q == "s":
+            return max(64, n) * CY, 0.0
+        if two:
+            return max(64, n * (1 if any(SCRATCH[x[1][0][0]][0] == "psum" for x in ins) else 2)) * CY, 0.0
+        return max(64, n * (1 if any(wide) else 0.5)) * CY, 0.0
+
+    def add(q, k, f, outs, ins, two=False, **kw):
+        r, w = [], []
+        for x in ins:
+            if isinstance(x, tuple):
+                r += x[1]
+        for x in outs:
+            if len(x) == 5:
+                w += x[3]
+                r += x[4]
+            else:
+                w += x[1]
+        c, l = span(q, k, outs, ins, two)
+        m = "sc" if outs and len(outs[0]) == 5 else "ga" if ins and len(ins[0]) == 5 else ""
+        o = {"q": q, "k": k, "f": f, "r": r, "w": w, "c": c, "l": l, "m": m,
+             "tag": q + (w[0][0] + tag[0] + str(w[0][1] // 1024 % 3) if w else tag[0])}
+        o.update(kw)
+        ops.append(o)
+
+    def ap(x):
+        return x[0] if isinstance(x, tuple) else x
+
+    def cp(o, i):
+        add("v", "c", lambda e: e.tensor_copy(o[0], i[0]), [o], [i])
+
+    def tt(o, a, b, op):
+        add("v", "c", lambda e: e.tensor_tensor(o[0], a[0], b[0], op), [o], [a, b], True)
+
+    def ts(o, a, s1, op0, s2=None, op1=None):
+        if op1 is None:
+            add("v", "c", lambda e: e.tensor_scalar(o[0], a[0], ap(s1), None, op0), [o], [a, s1])
+        else:
+            add("v", "c", lambda e: e.tensor_scalar(o[0], a[0], ap(s1), ap(s2), op0, op1), [o], [a, s1, s2])
+
+    def scan(o, d0, d1, init, op0, op1):
+        add("v", "c", lambda e: e.tensor_tensor_scan(o[0], d0[0], d1[0], ap(init), op0, op1), [o], [d0, d1, init])
+
+    def vtr(o, i):
+        add("v", "c", lambda e: e.transpose(o[0], i[0]), [o], [i])
+
+    def recip(o, i):
+        add("v", "c", lambda e: e.reciprocal(o[0], i[0]), [o], [i])
+
+    def act(o, i, f, bias=0.0, scale=1.0):
+        add("s", "c", lambda e: e.activation(o[0], i[0], f, bias=ap(bias), scale=ap(scale)), [o], [i, bias, scale])
+
+    def move(q, o, i):
+        if q == "v":
+            cp(o, i)
+        else:
+            act(o, i, AF.Copy)
+
+    def mm(o, l, r, start, stop):
+        add("t", "c", lambda e: e.matmul(o[0], l[0], r[0], start, stop), [o], [l, r])
+
+    def iota(o, pat, base, ch, small=True):
+        if small:
+            add("g", "c", lambda e: e.iota(o[0], pat, base, ch, allow_small_or_imprecise_dtypes=True), [o], [])
+        else:
+            add("g", "c", lambda e: e.iota(o[0], pat, base, ch), [o], [])
+
+    def gfill(o, c):
+        iota(o, [[0, o[1][0][2] - o[1][0][1]]], c, 0)
+
+    def asel(o, i, pat, base, ch, op, fill):
+        add("g", "c", lambda e: e.affine_select(o[0], i[0], pat, op, fill, base, ch), [o], [i])
+
+    def load(q, o, src, part=None):
+        if part is not None:
+            n, a, b = o[1][0]
+            o = (o[0], [(n, a + part, a + part + 1)], o[2])
+        add(q, "d", lambda e: e.dma_start(o[0], src), [o], [])
+
+    def store(q, dst, i):
+        add(q, "d", lambda e: e.dma_start(dst, i[0]), [], [i])
+
+    def dcopy(q, o, i):
+        add(q, "d", lambda e: e.dma_start(o[0], i[0]), [o], [i])
+
+    def send(x, sign, sn, s0, dn, d0, d1=1, d2=N, k=1):
+        sem = "arr%d" % x
+        tr, used = [], []
+        for d in range(d1, d2):
+            dst = T.cores[(rank + sign * d) % N]
+            rid, pid = topo.addr(dst, core)
+            en = [e for e in topo.engines(core, dst) if e not in used][:k]
+            used += en
+            tr.append(RemoteDMATransfer(
+                dst_ids=[DstId(rid=rid, pnc=pid)], dma_engine_mask=sum(1 << e for e in en), remote_sem=T.sem[sem],
+                src=T[sn][:, s0 + (d - 1) * G:s0 + d * G], dst=T[dn][:, d0 + (d - 1) * G:d0 + d * G]))
+        n = (d2 - d1) * k
+        add("g", "r", lambda e: e.remote_dma_fused(tr, local_sem=T.sem["sent"]), [], [v(sn, s0, s0 + GW)], n=n)
+        ops[-1]["after"] = sends[-1:]
+        sends.append(len(ops) - 1)
+        add("x", "x", None, [v(dn, d0 + (d1 - 1) * G, d0 + (d2 - 1) * G)], [], sem=sem, n=n)
+        if k > 1 and d1 == 1:
+            ops[-1]["l"] = TX - 1.0
+
+    def cmat(i, k=128):
+        return v("cm", i * 128, (i + 1) * 128, p=(0, k))
+
+    def sel(x):
+        return v("sel", x * 128, (x + 1) * 128)
+
+    h = (0, 64)
+
+    def spread(o, s, a, b, start=True, stop=True):
+        mm(o, v("ex", s * 128, (s + 1) * 128, p=h), v("m8h", a, b, p=h), start, stop)
+
+    P16 = v("pcf", 0, 1)
+    BET = v("bet", 0, 1)
+
+    load("y", v("t64", 0, 128, p=h), T.ti[:])
+    load("s", v("t64", 128, 256, p=h), T.kd[:])
+    load("y", v("sni", p=(16, 128)), T.snd[0:112, :], 0)
+    load("s", v("sni", p=(0, 16)), T.snd[112:128, :], 1)
+    load("y", v("ash", p=(16, 128)), T.a0[0:112, :], 0)
+    load("s", v("ash", p=(0, 16)), T.a0[112:128, :], 1)
+    load("y", v("cai"), T.ca[:])
+    load("s", BET, T.be[:])
+    for s, src in ((XT, T.ti[:, 0:384]), (XK, T.kd[:, 0:384]), (XU0, T.us[:, 0:384]), (XU1, T.us[:, 384:768]),
+                   (XC, T.cl[:]), (XL0, T.lp[:, 0:384]), (XL1, T.lp[:, 384:768]), (XL2, T.lp[:, 640:1024])):
+        load("y", v("m8", p=(8 * s, 8 * s + 8)), src, s)
+    load("y", v("kw", 16, 2064), T.k0[:])
+    load("y", v("mb", p=(0, 8)), T.bg[:])
+    load("y", v("aw", 0, E), T.a0[:])
+
+    iota(v("pci", 0, 1), [[0, 1]], 0, 1, False)
+    iota(v("ji", 0, 128), [[1, 128]], 128, -2, False)
+    iota(v("mk8", 8, 16), [[2, 8]], 0, 0)
+    iota(v("mc"), [[0, 8], [1, 16]], 0, 0)
+    asel(v("mc"), v("mc"), [[-16, 8], [0, 16]], 0, 1, OP.is_ge, -2.0)
+    asel(v("mc"), v("mc"), [[16, 8], [0, 16]], 15, -1, OP.is_ge, -2.0)
+    iota(v("exv", p=h), [[-1, 8], [0, 16]], 0, 1)
+    iota(v("r16"), [[0, 12], [1, 16]], 0, 0)
+    iota(v("ty", 0, 33), [[1, 33]], 0, 0)
+    iota(v("wc", 16, 28), [[-16, 12]], 95, 0)
+    iota(v("dum", 64, 76), [[16, 12]], 0, 0)
+    iota(v("thr", M, 2 * M), [[-1, M]], 95, 0)
+
+    ts(v("pci", 1, 2), v("pci", 0, 1), 15, OP.bitwise_and)
+    ts(v("pci", 2, 3), v("pci", 0, 1), 14, OP.bitwise_and)
+    cp(v("pcf", 0, 2), v("pci", 1, 3))
+    ts(v("ji", 128, 256), v("ji", 0, 128), 127, OP.bitwise_and)
+    for i, c in ((E0, 16), (E1, 17), (U0, 0), (U1, 1)):
+        ts(cmat(i), v("ji", 128, 256), float(c), OP.is_equal)
+    ts(v("mk8", 0, 8), v("mk8", 8, 16), v("pcf", 1, 2), OP.is_equal)
+    for x in range(8):
+        ts(sel(x), v("mc"), float(x), OP.is_equal)
+
+    ts(v("t64", 256, 384, p=h), v("t64", 0, 128, p=h), 8.0, OP.mult)
+    cp(v("snu"), v("sni"))
+    tt(v("t64", 0, 128, p=h), v("t64", 256, 384, p=h), v("t64", 128, 256, p=h), OP.add)
+    ts(v("t64", 384, 512, p=h), v("t64", 0, 128, p=h), 63, OP.bitwise_and)
+    cp(v("h64", 128, 256, p=h), v("t64", 384, 512, p=h))
+    tt(v("h64", 0, 128, p=h), v("t64", 0, 128, p=h), v("t64", 384, 512, p=h), OP.subtract)
+
+    def digits(a, b, bankn, dst):
+        mm(v(bankn, 0, 128), cmat(a, 64), v("h64", 0, 128, p=h), True, False)
+        mm(v(bankn, 0, 128), cmat(b, 64), v("h64", 128, 256, p=h), False, True)
+        cp(v("dg"), v(bankn, 0, 128))
+        for x in range(8):
+            ts(v(dst, 128 * x, 128 * x + 128), v("dg"), v("mk8", x, x + 1), OP.mult)
+
+    act(v("fb", GW, 2 * GW), ind(v("ash"), v("snu")), AF.Copy)
+    digits(E0, E1, "p0", "tks")
+    cp(v("fb", 0, 448), ind(v("tks"), v("snu", 0, 28)))
+    act(v("fb", 448, GW), ind(v("tks"), v("snu", 28, 56)), AF.Copy)
+    send(0, 1, "fb", 0, "tkw", E)
+    send(1, 1, "fb", GW, "aw", E)
+
+    digits(U0, U1, "p1", "tkw")
+    cp(v("cu"), v("cai"))
+    for x in range(8, 16):
+        ts(sel(x), v("mc"), float(x), OP.is_equal)
+    cp(v("m8h", p=h), v("m8", p=h))
+    for s in range(8):
+        ts(v("ex", s * 128, (s + 1) * 128, p=h), v("exv", p=h), float(8 * s), OP.is_equal,
+           -8.0 if s == XT else 1.0, OP.mult)
+    ts(v("ex32", p=(0, 8)), v("exv", p=(0, 8)), 0.0, OP.is_equal)
+    cp(v("mbf", p=(0, 8)), v("mb", p=(0, 8)))
+    ts(v("c1"), v("cai"), 1.0, OP.add)
+    ts(cmat(ONES), v("mc"), 0.0, OP.is_ge)
+    ts(cmat(TRI), v("mc"), P16, OP.is_ge, 256.0, OP.mult)
+    ts(cmat(R15), v("mc"), 0.0, OP.is_ge, -1.0, OP.mult)
+    ts(v("m8h", p=(8 * XK, 8 * XK + 8)), v("m8h", p=(8 * XK, 8 * XK + 8)), 8.0, OP.mult, 1.0, OP.add)
+    spread(v("p5", 0, 384), XU0, 0, 384)
+    spread(v("p6", 0, 384), XU1, 0, 384)
+    spread(v("p4", 0, 384), XC, 0, 384)
+    act(v("urep", 0, 384), v("p5", 0, 384), AF.Copy)
+    act(v("urep", 384, 768), v("p6", 0, 384), AF.Copy)
+    ts(v("oh"), v("p4", 0, 384), P16, OP.is_equal)
+    act(v("oh7"), v("oh"), AF.Identity, 7.0, -1.0)
+    spread(v("p5", 0, 384), XL0, 0, 384)
+    spread(v("p6", 0, 384), XL1, 0, 384)
+    spread(v("p4", 0, 256), XL2, 128, 384)
+    act(v("lw", 8, 392), v("p5", 0, 384), AF.Identity, 1.0)
+    act(v("lw", 392, 776), v("p6", 0, 384), AF.Identity, 1.0)
+    act(v("lw", 776, E + 8), v("p4", 0, 256), AF.Identity, 1.0)
+    ln2 = math.log(2.0)
+    ts(v("wc", 32, 44), v("wc", 16, 28), P16, OP.subtract)
+    act(v("wc", 0, 12), v("wc", 32, 44), AF.Exp, 0.0, ln2)
+    ops[-1]["c"] += 1.5
+    ops[-1]["r"] += v("fb", 0, 2 * GW)[1] + v("thr", M, 2 * M)[1]
+    ops[-1]["w"] += v("thr", 2 * M - 1, 2 * M)[1]
+    act(v("thr", M, 2 * M), v("thr", M, 2 * M), AF.Exp, 0.0, ln2)
+    ts(v("th"), v("r16"), P16, OP.is_equal, 2.5, OP.mult)
+    ts(v("rst"), v("r16"), 0.0, OP.not_equal)
+    ts(v("big"), v("r16"), 0.0, OP.is_equal, 1.0e6, OP.mult)
+    for a, c in ((0, 16 + W), (16, 2064), (32, 1 + W), (48, 2049)):
+        ts(v("dum", a, a + 12), v("dum", 64, 76), P16, OP.add, float(c), OP.add)
+    ts(v("pcf", 2, 3), P16, 0.0, OP.is_equal, -5000.0, OP.mult)
+    tt(v("thr", 0, M), v("thr", M, 2 * M), v("th"), OP.mult)
+    row = [[-1, 128]]
+    asel(cmat(DM), cmat(R15), row, -1, 1, OP.is_equal, 0.0)
+    asel(cmat(DM), cmat(DM), row, 0, 1, OP.not_equal, 1.0)
+    asel(cmat(DL), cmat(ONES), row, 1, 1, OP.is_equal, 0.0)
+    asel(cmat(DL), cmat(DL), row, 0, 1, OP.not_equal, -1.0)
+    asel(cmat(DU), cmat(R15), row, 0, 1, OP.is_gt, 0.0)
+    asel(cmat(DU), cmat(DU), row, 0, 1, OP.not_equal, 1.0)
+    asel(cmat(R15), cmat(R15), [[-16, 8], [0, 16]], -15, 1, OP.is_equal, 0.0)
+    gfill(v("ty", 232, 463), 0)
+    gfill(v("ty", 464, 695), 1)
+    gfill(v("hi", 0, 64), 0)
+    gfill(v("kw", 0, 16), 0)
+    gfill(v("kw", 2064, KWID), 0)
+    gfill(v("zb", 0, RW), 0)
+    gfill(v("cm", NI * 128, (NUSH + 1) * 128), 0)
+    for i, bases in ((NI, (0,)), (NSH, (16, -112)), (NUSH, (-16, 112))):
+        for b in bases:
+            asel(cmat(i), cmat(i), row, b, 1, OP.not_equal, -1.0)
+    gfill(v("lw", 0, 8), 0)
+    gfill(v("lw", E + 8, E + 16), 0)
+
+    def ratio_table():
+        for n in range(1, 7):
+            ts(v("ty", 232 + n, 463, 7), v("ty", 0, 33), BET, OP.mult, -1.0 / (7 - n), OP.mult)
+        scan(v("ty", 696, 927), v("ty", 232, 463), v("ty", 464, 695), 0.0, OP.mult, OP.add)
+        ts(v("hi", 64, 128), v("hi", 0, 64), v("ty", 926, 927), OP.add)
+        scan(v("hi", 128, 161), v("hi", 64, 97), v("hi", 0, 33), 1.0, OP.mult, OP.add)
+        recip(v("hi", 176, 177), v("hi", 160, 161))
+        scan(v("hi", 192, 256), v("hi", 64, 128), v("hi", 0, 64), v("hi", 176, 177), OP.mult, OP.add)
+
+    def ratio_fill():
+        for b in range(32):
+            act(v("rt", b, 2048, 32), v("hi", 192, 256), AF.Identity, 0.0, v("ty", 702 + 7 * b, 703 + 7 * b))
+            ops[-1]["w"] = [("rt", b, b + 1)]
+        act(v("rt", 0, 1), v("hi", 0, 1), AF.Copy)
+
+    def tk_gather(q, t, i0, i1):
+        lo = (t % 2) * M
+        move(q, v("tg", 16 * i0, 16 * i1), ind(v("tkw"), v("cu", lo + i0, lo + i1)))
+
+    def tk_extract(t, i0, i1):
+        lo = (t % 2) * M
+        o = v("p3", i0, i1)
+        spread(o, XT, lo + i0, lo + i1, True, False)
+        for k in range(16):
+            mm(o, sel(k), v("tg", 16 * i0 + k, 16 * i1, 16), False, k == 15)
+
+    def bins(t):
+        lo = (t % 2) * M
+        X, Y = v("p3", 0, M), v("p3", M, 2 * M)
+        spread(Y, XK, lo, lo + M)
+        y = v("bf", 3 * M, 4 * M)
+        a, b, kc, li = [v("bi", j * M, (j + 1) * M) for j in range(4)]
+        xi, b1 = v("xi", lo, lo + M), v("b1", t * M, (t + 1) * M)
+        if t == 0:
+            ts(y, X, -1.0, OP.mult, 7.0, OP.add)
+        else:
+            act(y, X, AF.Identity, 7.0, -1.0)
+        cp(xi, X)
+        tt(a, X, y, OP.max)
+        ts(kc, xi, 7, OP.bitwise_and)
+        ts(b, a, 2, OP.arith_shift_right, 1984, OP.bitwise_and)
+        tt(Y, kc, Y, OP.add)
+        ts(li, a, 3, OP.arith_shift_right)
+        tt(b1, b, Y, OP.add)
+        cp(v("l16"), li)
+        ts(v("binu", t * M, (t + 1) * M), b1, -1.0, OP.add)
+        mm(Y, cmat(DL), v("l16"), True, True)
+        mm(X, cmat(R15), v("l16"), True, True)
+
+    def steps(t):
+        lo = (t % 2) * M
+        mm(v("p7", 0, M), cmat(DM), v("c1", lo, lo + M), True, True)
+        mm(v("p7", M, 2 * M), cmat(DM), v("b1", t * M, (t + 1) * M), True, True)
+
+    def lags(t):
+        ts(v("dlt", t * M, (t + 1) * M), v("p3", M, 2 * M), v("pcf", 2, 3), OP.add, 1024.0, OP.add)
+        act(v("e15", t * M, (t + 1) * M), v("p3", 0, M), AF.Exp, 0.0, BET)
+
+    def k_gather(q, t, i0, i1):
+        move(q, v("kg", 16 * i0, 16 * i1), ind(v("kw", 16, 2064), v("binu", t * M + i0, t * M + i1)))
+
+    def elected(j, s, i0, i1):
+        a, b = j * M + i0, j * M + i1
+        tt(v("hd", a, b), v("p7", a, b), v("th", i0, i1), OP.mult)
+        mm(v("p2", i0, i1), cmat(ONES), v("hd", a, b), True, True)
+        cp(v("rep", s * M + i0, s * M + i1), v("p2", i0, i1))
+        li = v("p1", 400 + i0 // 16, 400 + i1 // 16)
+        for x in range(16):
+            mm(li, sel(x), v("hd", a + x, b, 16), x == 0, x == 15)
+        cp(v("lst", 16 * s + i0 // 16, 16 * s + i1 // 16), li)
+
+    def elect(t, i0, i1, w, x):
+        w16 = v("w16", (t % 2) * M + i0, (t % 2) * M + i1)
+        cp(w16, w)
+        mm(x, cmat(ONES), w16, False, True)
+        mm(v("p1", i0, i1), cmat(TRI), w16, True, True)
+        tt(v("th", i0, i1), x, v("urep", t * M + i0, t * M + i1), OP.mult)
+        tt(v("th", i0, i1), v("p1", i0, i1), v("th", i0, i1), OP.is_gt)
+        elected(0, t % 2, i0, i1)
+
+    def first_of(j, s):
+        dum = 16 * j
+        lst = v("lst", 16 * s, 16 * s + 12)
+        if j == 1:
+            elected(1, s, 0, M)
+        for y in range(12):
+            z = v("zz", y * M + 16 * y, (y + 1) * M)
+            ts(z, v("rep", s * M + 16 * y, (s + 1) * M), v("lst", 16 * s + y, 16 * s + y + 1), OP.is_equal,
+               v("wc", y, y + 1), OP.mult)
+            mm(v("p4", 16 * y, M), cmat(ONES), z, y == 0, y == 11)
+        tt(v("sm", 0, 12), lst, v("dum", dum + 32, dum + 44), OP.subtract)
+        tt(v("fl", 0, M), v("p4", 0, M), v("thr", 0, M), OP.is_lt)
+        scan(v("fl", M, 2 * M), v("rst"), v("fl", 0, M), 0.0, OP.mult, OP.add)
+        tt(v("sm", 16, 28), v("fl", M + 15, 2 * M, 16), v("sm", 0, 12), OP.mult)
+        tt(v("sm", 32, 44), v("sm", 16, 28), v("dum", dum, dum + 12), OP.add)
+        cp(v("offs", 16 * j, 16 * j + 12), v("sm", 32, 44))
+
+    def ratios(t, c):
+        a = (t % 2) * C + 1024 * c
+        act(v("rg", a, a + 1024), ind(v("rt"), v("dlt", t * M + 64 * c, t * M + 64 * c + 64)), AF.Copy)
+
+    def lam(t, c):
+        a, so = 1024 * c, 1024 * ((3 * t + c) % 2)
+        o0 = t * M + 64 * c
+        for b in range(0, 1024, LW):
+            scan(v("so", so + b, so + b + LW), v("rg", (t % 2) * C + a + b, (t % 2) * C + a + b + LW),
+                 v("pr", t * C + a + b, t * C + a + b + LW), 0.0, OP.mult, OP.add)
+        tt(v("ylf", o0, o0 + 64), v("so", so + 15, so + 1024, 16), v("e15", o0, o0 + 64), OP.mult)
+        if c == 2:
+            store("y", T.yl[:, t * M:(t + 1) * M], v("ylf", t * M, (t + 1) * M))
+
+    def least(t):
+        f0, f1, f2 = [v("bf", j * M, (j + 1) * M) for j in range(3)]
+        ts(f0, v("w16", t * M, (t + 1) * M), 16.0, OP.mult, P16, OP.add)
+        vtr(f1, f0)
+        scan(f2, v("big"), f1, 0.0, OP.add, OP.min)
+        vtr(v("p3", 0, M), f2)
+        tt(v("rec"), f0, v("p3", 0, M), OP.is_equal)
+
+    def candidates(t):
+        lo = t * M
+        up, flag = v("up"), v("bf", 4 * M, 5 * M)
+        X, y, xi = v("p3", 0, M), v("p3", M, 2 * M), v("xi", lo, lo + M)
+        rep, lw, c1 = v("rep", lo, lo + M), v("lw", 8 + lo, 8 + lo + M), v("c1", lo, lo + M)
+        ts(y, rep, 0.0, OP.is_equal)
+        ts(v("offs", 32, 44), v("lst", 16 * t, 16 * t + 12), 1025.0, OP.min, 7.0, OP.add)
+        tt(y, y, lw, OP.mult)
+        tt(lw, y, rep, OP.add)
+        cp(up, ind(v("lw"), v("offs", 32, 44)))
+        mm(y, cmat(DU), v("rec"), True, True)
+        for k in range(16):
+            mm(v("p3", 400, 412), sel(k), v("up", k, M, 16), k == 0, k == 15)
+        ts(v("offs", 48, 60), v("p3", 400, 412), 0.0625, OP.mult, -1.0, OP.add)
+        tt(y, y, up, OP.min)
+        ts(flag, y, 0.0, OP.max)
+        tt(y, up, c1, OP.subtract)
+        tt(y, y, flag, OP.mult)
+        tt(c1, y, c1, OP.add)
+        act(v("tg", 0, M), ind(v("tkw"), v("offs", 48, 60)), AF.Copy)
+        spread(X, XT, lo, lo + M, True, False)
+        mm(X, cmat(ONES), v("tg", 0, M), False, True)
+        ts(v("cu", lo, lo + M), c1, -1.0, OP.add)
+        tt(X, X, xi, OP.subtract)
+        tt(X, X, flag, OP.mult)
+        tt(X, X, xi, OP.add)
+        bins(t + 2)
+        lags(t + 2)
+
+    ratio_table()
+    for c in range(3):
+        tk_gather("v", 0, 64 * c, 64 * c + 32)
+        tk_gather("s", 0, 64 * c + 32, 64 * c + 64)
+        tk_extract(0, 64 * c, 64 * c + 64)
+    bins(0)
+    steps(0)
+    for c in range(3):
+        act(v("kg", 1024 * c, 1024 * c + 1024), ind(v("aw", 0, W), v("cu", 64 * c, 64 * c + 64)), AF.Copy)
+    lags(0)
+    for a in range(RW, ZW, RW):
+        b = min(a + RW, ZW)
+        dcopy("y", v("zb", a, b), v("zb", 0, b - a))
+        ops[-1]["r"] += v("binu", 0, M)[1]
+
+    for t in range(R):
+        lo, a0, r0 = (t % 2) * M, t * W, t * RW
+        last, tag[0] = t == R - 1, str(t)
+        XA, XB = v("p2", 256, 384), v("p0", 448, 512)
+        mm(XA, v("ex32", p=(0, 8)), v("mbf", lo, lo + 128, p=(0, 8)), True, False)
+        for c in range(3):
+            a = t * C + 1024 * c
+            if t == 0:
+                tt(v("pr", a, a + 1024), ind(v("kw", 16, 2064), v("binu", 64 * c, 64 * c + 64)),
+                   v("kg", a, a + 1024), OP.mult)
+            elif c == 0:
+                tt(v("pr", a, a + 1024), ind(v("aw", a0, a0 + W), v("cu", lo, lo + 64)), v("kg", 0, 1024), OP.mult)
+            else:
+                for hf in range(2):
+                    b, i0 = 1024 * c + 512 * hf, lo + 64 * c + 32 * hf
+                    mm(v("p%d" % (5 + hf)), cmat(NI), v("kg", b, b + 512), True, True)
+                    act(v("ag", b - 1024, b - 512), ind(v("aw", a0, a0 + W), v("cu", i0, i0 + 32)), AF.Identity,
+                        0.0, -1.0)
+                    tt(v("pr", t * C + b, t * C + b + 512), v("p%d" % (5 + hf)), v("ag", b - 1024, b - 512), OP.mult)
+            for k in range(16):
+                mm(v("p0", 64 * c, 64 * c + 64) if c < 2 else v("p4", 0, 64), sel(k), v("pr", a + k, a + 1024, 16),
+                   k == 0, k == 15)
+        elect(t, 0, 128, v("p0", 0, 128), XA)
+        mm(XB, v("ex32", p=(0, 8)), v("mbf", lo + 128, lo + M, p=(0, 8)), True, False)
+        elect(t, 128, M, v("p4", 0, 64), XB)
+        if t == 0:
+            for c in range(3):
+                tk_gather("s", 1, 64 * c, 64 * c + 64)
+            ratio_fill()
+        for c in range(3):
+            ratios(t, c)
+        first_of(0, t % 2)
+        cp(ind(v("zb", r0, r0 + RW), v("offs", 0, 12)), v("oh", lo, lo + M))
+        send(2 + t, -1, "zb", r0 + 16 + E, "rv", t * GW, 1, 5, 2)
+        send(9 + t, -1, "zb", r0 + 16 + E, "rv", t * GW, 5, N, 2)
+        if t == 0:
+            tk_extract(1, 0, M)
+        if not last:
+            first_of(1, 2)
+            if t > 0:
+                steps(t + 1)
+            tt(v("kt"), ind(v("kw"), v("offs", 16, 28)), v("oh7", lo, lo + M), OP.min)
+            tt(ind(v("kw"), v("offs", 16, 28)), v("kt"), v("oh", lo, lo + M), OP.add)
+        for hf in range(2):
+            o = v("p%d" % (5 + hf))
+            mm(o, cmat(NI if last else NSH), v("aw", a0 + 512 * hf, a0 + 512 * hf + 512), True, False)
+            mm(o, cmat(NI if last else NSH), v("zb", r0 + 16 + 512 * hf, r0 + 16 + 512 * hf + 512), False, False)
+        if not last:
+            if t == 0:
+                bins(1)
+                steps(1)
+                lags(1)
+            for c in range(3):
+                k_gather("s", t + 1, 64 * c, 64 * c + 64)
+        else:
+            for c in range(3):
+                lam(t, c)
+        for d in range(N - 1):
+            pl = PL + d * E
+            cp(ind(v("zb", pl, pl + E), v("snu", 8 * d, 8 * d + 8)), v("rv", t * GW + d * G, t * GW + (d + 1) * G))
+            for hf in range(2):
+                mm(v("p%d" % (5 + hf)), cmat(NUSH if last else NI), v("zb", pl + 512 * hf, pl + 512 * hf + 512),
+                   False, d == N - 2)
+        if last:
+            for hf in range(2):
+                o = v("yaf", 512 * hf, 512 * hf + 512)
+                ts(o, v("p%d" % (5 + hf)), -1.0, OP.mult, 15.0, OP.min)
+                store("y" if hf == 0 else "s", T.ya[:, 512 * hf:512 * hf + 512], o)
+            break
+        ts(v("ash", 0, 512), v("p5"), 15.0, OP.add, 0.0, OP.max)
+        act(v("ash", 512, E), v("p6"), AF.Relu, 15.0)
+        f0 = (t + 2) * GW
+        ts(v("fb", f0, f0 + 448), ind(v("ash"), v("snu", 0, 28)), -1.0, OP.mult, 15.0, OP.add)
+        act(v("fb", f0 + 448, f0 + GW), ind(v("ash"), v("snu", 28, 56)), AF.Identity, 15.0, -1.0)
+        send(6 + t, 1, "fb", f0, "aw", a0 + W + E)
+        for hf in range(2):
+            mm(v("p%d" % (5 + hf)), cmat(NUSH), v("ash", 512 * hf, 512 * hf + 512), True, True)
+            act(v("aw", a0 + W + 512 * hf, a0 + W + 512 * hf + 512), v("p%d" % (5 + hf)), AF.Identity, 15.0)
+        if t < 2:
+            least(t)
+            candidates(t)
+        for c in range(3):
+            lam(t, c)
+    emit(g, T, ops)

@@ -1,4 +1,3 @@
-import math
 from concourse.bass import DstId, RemoteDMATransfer
 from concourse.mybir import AluOpType as OP, ActivationFunctionType as AF
 
@@ -6,102 +5,214 @@ N, E, G, M, R = 8, 1024, 128, 192, 4
 W = E + (N - 1) * G
 GW = (N - 1) * G
 C = 16 * M
-RW = 2144
+SP = 208
+RW = SP + W
 PL = 4 * RW
 ZW = PL + 7 * E
-KWID = 16 + 2048 + M
+KWID = SP + 2048
+AW = 16 + W
+BIG = 4096.0
 BF, F32, F16, I32, U16 = "bfloat16", "float32", "float16", "int32", "uint16"
+
+(NI, NSH, NUSH, ID, ID64, EM, EL, ONES, NON, TRS, DM, DU, DLP, DLD, ELM, VALM, UPM, UT, KK, TRI) = range(20)
+NON32, ID32, XBM = range(3)
+XU0, XU1, XC, XT, XL0, XL1, XL2, XB, XK = range(9)
+(P16, NXT, P12, P3, P1, KC8, K18, TCOL, NPAR, SGN, VALC, LT4, C15, NDZ, DCON, PQ, TB, MMUL, MADD, EAT,
+ EBY) = range(21)
+
+WHOLE = ((1, N, 1),)
+RAISES = ((1, 3, 4), (3, 5, 4), (5, 7, 4), (7, N, 8))
+FORTH = ((1, 5, 2), (5, N, 2))
+PIECES = (((0, 32, "v"), (32, 64, "v"), (64, 96, "v"), (96, 128, "v"), (128, 160, "v"), (176, M, "s"), (160, 176, "v")),
+          ((0, 64, "v"), (64, 96, "s"), (96, 128, "s"), (128, 160, "s"), (160, 180, "s"), (180, M, "s")))
+SUMS = ((0, 64), (64, 128), (128, M))
+PARTS = ((0, 128), (128, M))
+LW = 512
+KPOS = 3
 
 SCRATCH = {}
 for _n, _w, _d in (
-        ("zb", ZW, BF), ("aw", R * W, BF), ("ash", E, BF), ("tks", E, BF), ("tkw", W, BF), ("fb", 5 * GW, BF),
-        ("rv", R * GW, BF), ("kw", KWID, BF), ("kg", C, BF), ("tg", C, BF), ("ag", 2048, BF), ("pr", R * C, BF), ("rg", 2 * C, F32),
-        ("so", 2048, F32), ("rt", 2048, F32), ("lw", E + 16, F32), ("yaf", E, F32), ("ylf", R * M, F32),
-        ("e15", R * M, F32), ("t64", 512, I32), ("h64", 256, F16), ("dg", 128, BF), ("sni", 56, I32),
-        ("snu", 56, U16), ("cai", 2 * M, I32), ("cu", 2 * M, U16), ("c1", 2 * M, F16), ("m8", 384, I32),
-        ("m8h", 384, F16), ("mb", 384, I32), ("mbf", 384, F32), ("ex", 8 * 128, BF), ("ex32", 128, F32),
-        ("exv", 128, BF), ("bet", 8, F32), ("urep", R * M, F32), ("oh", 2 * M, BF), ("ji", 256, I32),
-        ("pci", 8, I32), ("pcf", 8, F32), ("mk8", 16, F32), ("mc", 128, BF), ("cm", 13 * 128, BF),
-        ("sel", 16 * 128, BF), ("r16", M, F32), ("thr", 2 * M, F32), ("rst", M, BF), ("big", M, F32),
-        ("wc", 64, F32), ("dum", 80, F32), ("w16", 2 * M, F16), ("th", M, F32), ("hd", 2 * M, F16),
-        ("rep", 3 * M, F16), ("lst", 48, F32), ("zz", 12 * M, BF), ("fl", 2 * M, BF), ("sm", 48, F32),
-        ("offs", 64, U16), ("kt", M, BF), ("oh7", 2 * M, BF), ("bi", 4 * M, I32), ("bf", 5 * M, F32), ("b1", R * M, F16),
-        ("l16", M, F16), ("binu", R * M, U16), ("xi", 2 * M, I32), ("up", M, F16), ("dlt", R * M, U16), ("rec", M, BF), ("ty", 4 * 232, F32),
-        ("hi", 4 * 64, F32)):
+        ("zb", ZW, BF), ("aw", R * AW, BF), ("ash", E, BF), ("tks", E, BF), ("tkw", AW, BF), ("fb", 5 * GW, BF),
+        ("rv", R * GW, BF), ("kw", KWID, BF), ("kg", C + M, BF), ("tg", C, BF), ("ag", C, BF), ("pr", R * C, BF),
+        ("rg", 2 * C, F32), ("so", 2048, F32), ("rt", 2048, F32), ("lw", E + 16, F32), ("yaf", E, F32),
+        ("ylf", R * M, F32), ("e15", 2 * M, F32), ("t128", 128, I32), ("hl", 256, BF), ("dg", 256, BF),
+        ("sni", 56, I32), ("snu", 56, U16), ("cai", 2 * M, I32), ("cu", 2 * M, U16), ("c1", 2 * M, F16),
+        ("m8", 384, I32), ("m8h", 384, F16), ("mbf", 384, F32), ("ex", 8 * 128, BF), ("exv", 2 * 128, BF),
+        ("bet", 8, F32), ("urep", R * M, BF), ("oh", 2 * M, BF), ("ji", 256, I32), ("pci", 8, I32),
+        ("pcf", 24, F32), ("mk4", 8, F32), ("mc", 128, BF), ("cm", 20 * 128, BF), ("cf", 3 * 128, F32), ("w16", M, F16),
+        ("ub", R * M, F32), ("pn", 2 * M, BF), ("en", 2 * M, F32), ("wn", M, F16), ("oi", 16, I32),
+        ("sel", 32 * 128, BF), ("r16", M, BF), ("mkc", M, BF), ("d0", M, BF), ("big", M, BF), ("d12", 16, F32),
+        ("w32", 2 * M, F32), ("wu", M, F32), ("hit", 2 * M, BF), ("hd", 3 * M, F16), ("rep", 2 * M, F16),
+        ("lst", 3 * M, F32), ("zz", 12 * M, BF), ("sc", M, F32), ("offs", 136, U16), ("kt", M, BF),
+        ("oh7", 2 * M, BF), ("ab", M, F32), ("qq", M, BF), ("bf", 2 * M, F32), ("b1", 2 * M, F16), ("l16", M, F16),
+        ("binu", 2 * M, U16), ("up", M, F16), ("tn", M, BF), ("dlt", 2 * M, U16), ("rec", M, BF),
+        ("flag", 3 * M, BF), ("tc", 2 * M, F16), ("tb", M, F16), ("ty", 4 * 120, F32), ("hi", 4 * 128, F32)):
     SCRATCH[_n] = ("sbuf", [128, _w], _d)
 for _b in range(8):
     SCRATCH["p%d" % _b] = ("psum", [128, 512], F32)
-NDMA = 40
-SEMAPHORES = ["cv", "cs", "ct", "cg", "sent"] + ["arr%d" % _i for _i in range(13)] + ["dm%d" % _i for _i in range(NDMA)]
+NDMA = 44
+NARR = 2 * len(WHOLE) + R * len(RAISES) + (R - 1) * len(FORTH)
+SEMAPHORES = ["cv", "cs", "ct", "cg", "sent"] + ["arr%d" % _i for _i in range(NARR)] + ["dm%d" % _i for _i in range(NDMA)]
 
-CY, PE, TX, HOP, PASSES = 0.00104, 0.00055, 4.5, 0.1, 2
-CASES = ((0.8, 0.67, 0.42, 0.7), (1.0, 1.0, 1.0, 1.0), (1.0, 1.0, 1.0, 1.5), (1.2, 1.33, 1.58, 1.3))
+CY, PE, CALL, WAY, ROW, HOP = 0.00104, 0.00055, 0.5, 1.9, 0.0205, 0.1
+CASES = ((0.8, 1.0, 1.0, 1.1, 0.1, 1.0, 1.0), (1.0, 1.15, 0.9, 1.2, 0.1, 1.2, 2.0), (1.15, 1.1, 1.45, 1.6, 0.15, 1.0, 2.5),
+         (1.1, 1.33, 0.6, 0.9, 0.07, 1.0, 2.0), (1.0, 0.75, 1.3, 1.0, 0.1, 1.5, 1.0))
+TRIES, STEPS, SLACK, PLAN = 5000, 600, 0.01, 1
 ORDER = {}
-LW = 256
-URGE = {'ga': 30, 'skg00': 8, 'skg10': 9, 'skg20': 7, 'skg01': 6, 'skg11': 6, 'skg21': 6, 'vlst20': 1, 'srt00': 8, 'gcma0': -1,
-        'vb100': -1, 'vp310': 1, 'vrec00': -2, 'stg02': -1, 'srg22': 8, 'vrep00': -1, 'gtya0': 30, 'vpr20': 1,
-        'voffs30': 1, 'gr16a0': 4, 'vxia0': -4, 'vbinua0': 30, 'vzz20': 2, 'vlw00': 4, 'vash10': 4, 'vzz10': -10,
-        'vpr11': -1, 'vpr30': -1, 'skga2': -10, 'vsm20': 1, 'gwca0': 15, 'skg12': -4}
-NI, NSH, NUSH, E0, E1, U0, U1, ONES, TRI, DM, DU, DL, R15 = range(13)
-XU0, XU1, XC, XT, XK, XL0, XL1, XL2 = range(8)
 
 
 def arrange(ops, pre):
     n = len(ops)
-    after = [[] for _ in range(n)]
-    for i in range(n):
-        for j in pre[i]:
-            after[j].append(i)
-    tail = [0.0] * n
+    queue = ["vstgyx".index(o["q"]) for o in ops]
+    wait = [[(j, 0.0 if (ops[i]["q"] == "t" and ops[j]["q"] == "t") or j in ops[i].get("after", ()) else 1.0)
+             for j in pre[i]] for i in range(n)]
+    rank, stage, k = [0.0] * n, [n] * n, 0
     for i in range(n - 1, -1, -1):
-        tail[i] = ops[i]["c"] + ops[i]["l"] + max([tail[j] + HOP for j in after[i]] + [0.0])
+        rank[i] += ops[i]["c"] + ops[i]["l"]
+        for j, h in wait[i]:
+            rank[j] = max(rank[j], rank[i] + (h * HOP if h else -ops[j]["l"]))
+    for i in range(n):
+        if ops[i]["k"] == "r" or ops[i].get("end"):
+            k += 1
+            todo = [i]
+            while todo:
+                j = todo.pop()
+                if stage[j] == n:
+                    stage[j] = k
+                    todo.extend(pre[j])
 
-    def place(seq, back):
-        start, busy = [0.0] * n, {}
-        for i in seq:
-            o, s = ops[i], 0.0
-            for j in (after[i] if back else pre[i]):
-                hop = 0.0 if (o["q"] == "t" and ops[j]["q"] == "t") else HOP
-                s = max(s, start[j] + ops[j]["c"] + (o["l"] if back else ops[j]["l"]) + hop)
-            if back and not after[i]:
-                s = o["l"]
-            if o["q"] != "x":
-                row, k = busy.setdefault(o["q"], []), 0
-                while k < len(row) and row[k][0] < s + o["c"] - 1e-9:
-                    s = max(s, row[k][1])
-                    k += 1
-                row.insert(k, (s, s + o["c"]))
-            start[i] = s
-        return start
-
-    def length(order, f, ga, sc, tx):
-        done, free = [0.0] * n, {}
-        for i in order:
-            o = ops[i]
-            s = free.get(o["q"], 0.0) if o["q"] != "x" else 0.0
-            for j in pre[i]:
-                s = max(s, done[j] + (0.0 if (o["q"] == "t" and ops[j]["q"] == "t") else HOP))
-            free[o["q"]] = s + o["c"] * f * (ga if o["m"] == "ga" else sc if o["m"] == "sc" else 1.0)
-            done[i] = free[o["q"]] + o["l"] * (tx if o["k"] == "x" else 1.0)
-        return max(done)
-
-    def ranked(worth):
-        w = [worth[i] + URGE.get(ops[i]["tag"], 0.0) for i in range(n)]
+    def place(key, case):
+        cost, lag, ws, _ = case
+        key = key[:]
         for i in range(n - 1, -1, -1):
-            w[i] = max([w[i]] + [w[j] + 1e-6 for j in after[i]])
-        return sorted(range(n), key=lambda i: (-w[i], i))
+            for j in pre[i]:
+                if key[j] <= key[i]:
+                    key[j] = key[i] + 1e-6
+        start, done, rows = [0.0] * n, [0.0] * n, [([], []) for _ in range(5)]
+        for i in sorted(range(n), key=lambda i: -key[i]):
+            s, c = 0.0, cost[i]
+            for j, h in ws[i]:
+                if done[j] + h > s:
+                    s = done[j] + h
+            if queue[i] < 5:
+                first, end = rows[queue[i]]
+                lo, k = 0, len(end)
+                while lo < k:
+                    if end[(lo + k) // 2] > s:
+                        k = (lo + k) // 2
+                    else:
+                        lo = (lo + k) // 2 + 1
+                while k < len(end) and first[k] < s + c - 1e-9:
+                    s = max(s, end[k])
+                    k += 1
+                first.insert(k, s)
+                end.insert(k, s + c)
+            start[i], done[i] = s, s + c + lag[i]
+        return sorted(range(n), key=lambda i: (start[i], i)), key
 
-    seq, best = ranked(tail), None
-    for _ in range(PASSES):
-        start = place(seq, False)
-        order = sorted(range(n), key=lambda i: (start[i], i))
-        end = sum(length(order, *m) / (m[0] * (m[1] + m[2] + 2)) for m in CASES)
-        if best is None or end < best[0]:
-            best = (end, order)
-        late = place(sorted(range(n), key=lambda i: (-start[i] - ops[i]["c"] - ops[i]["l"], -i)), True)
-        seq = ranked([late[i] + ops[i]["c"] for i in range(n)])
-    ORDER["end"] = best[0]
-    return best[1]
+    def waits(runs, step):
+        _, i, by, _ = runs[step % len(runs)]
+        pairs = []
+        while by[i] >= 0:
+            if by[i] not in pre[i]:
+                pairs.append((by[i], i))
+            i = by[i]
+        return pairs
+
+    def rerank(key):
+        order, full = place(key, cases[PLAN])
+        best, runs = worth(order)
+        seed = 4321
+        for step in range(TRIES):
+            pairs = waits(runs, step)
+            seed = (seed * 1103515245 + 12345) % 2147483648
+            u, w = pairs[(seed >> 8) % len(pairs)]
+            new, far = key[:], (seed >> 4) % 8 * 0.1 + 0.01
+            if full[w] > full[u]:
+                new[u] = key[u] + (1 if seed >> 20 & 1 else -1) * far * 4
+            elif seed >> 20 & 1:
+                new[w] = full[u] + far
+            else:
+                new[u] = full[w] - far
+            o, f = place(new, cases[PLAN])
+            end, r = worth(o)
+            if end < best + SLACK:
+                best, runs, order, key, full = end, r, o, new, f
+        return order
+
+    cases = []
+    for f, ga, sc, tx, hop, pe, call in CASES:
+        by = {"ga": f * ga, "sc": f * sc, "t": f * pe}
+        cost = [o["c"] * by.get(o["m"] or o["q"], f) if o["k"] == "c" else o["c"] + (call - 1) * (0.1, CALL)[o["k"] == "r"]
+                if o["k"] != "x" else 0.0 for o in ops]
+        cases.append((cost, [o["l"] * (tx if o["k"] == "x" else 1.0) for o in ops],
+                      [[(j, h * hop if h else -ops[j]["l"]) for j, h in w] for w in wait], f * (ga + sc + 2) + tx))
+
+    def length(order, case, a=0, old=None):
+        cost, lag, ws, _ = case
+        done, by = (old[3][:], old[2][:]) if a else ([0.0] * n, [-1] * n)
+        free, last, k = [0.0] * 6, [-1] * 6, a
+        while k and -1 in last[:5]:
+            k -= 1
+            i = order[k]
+            if queue[i] < 5 and last[queue[i]] < 0:
+                free[queue[i]], last[queue[i]] = done[i] - lag[i], i
+        for i in order[a:]:
+            q = queue[i]
+            s, b = free[q], last[q]
+            for j, h in ws[i]:
+                if done[j] + h > s:
+                    s, b = done[j] + h, j
+            by[i] = b
+            s += cost[i]
+            done[i] = s + lag[i]
+            if q < 5:
+                free[q], last[q] = s, i
+        end = max(done)
+        return end, done.index(end), by, done
+
+    def worth(order, a=0, old=(None,) * 9):
+        runs = [length(order, c, a, o) for c, o in zip(cases, old)]
+        return sum(r[0] / c[3] for r, c in zip(runs, cases)), runs
+
+    def refine(order):
+        best, runs = worth(order)
+        seed = 12345
+        for step in range(STEPS):
+            pairs = waits(runs, step)
+            seed = (seed * 1103515245 + 12345) % 2147483648
+            u, w = pairs[(seed >> 8) % len(pairs)]
+            a, b = order.index(u), order.index(w)
+            far = (seed >> 4) % 4
+            if seed >> 20 & 1:
+                while far and a > 0:
+                    a -= 1
+                    far -= queue[order[a]] == queue[w]
+                part, need = order[a:b + 1], {w}
+                for x in reversed(part):
+                    if x in need:
+                        need.update(pre[x])
+                new = [x for x in part if x in need] + [x for x in part if x not in need]
+            else:
+                while far and b < n - 1:
+                    b += 1
+                    far -= queue[order[b]] == queue[w]
+                part, need = order[a:b + 1], {u}
+                for x in part:
+                    if not need.isdisjoint(pre[x]):
+                        need.add(x)
+                new = [x for x in part if x not in need] + [x for x in part if x in need]
+            if new == part:
+                continue
+            trial = order[:a] + new + order[b + 1:]
+            end, r = worth(trial, a, runs)
+            if end < best + SLACK * (1 - step / STEPS):
+                best, runs, order = end, r, trial
+        return order
+
+    order = refine(rerank([rank[i] - 1000.0 * stage[i] for i in range(n)]))
+    ORDER["end"] = [r[0] for r in worth(order)[1]]
+    return order
 
 
 def emit(g, T, ops):
@@ -125,22 +236,21 @@ def emit(g, T, ops):
                 run[1].append(i)
         if o["k"] == "x":
             d.add(i - 1)
-        d.update(o.get("after", ()))
         pre.append(d)
         for (n, a, b) in o["w"]:
             log[n] = [x for x in log.get(n, []) if not (a <= x[0] and x[1] <= b)] + [(a, b, i, True)]
         for (n, a, b) in o["r"]:
             log.setdefault(n, []).append((a, b, i, False))
-    key = (len(ops), CY, PE, TX, HOP, PASSES)
+    key = len(ops)
     if key not in ORDER:
-        ORDER[key] = arrange(ops, pre)
+        ORDER[key] = arrange(ops, [d | set(o.get("after", ())) for d, o in zip(pre, ops)])
     order = ORDER[key]
     place = dict((i, p) for p, i in enumerate(order))
     deps = {}
     for i in order:
         o, best, keep = ops[i], {}, []
         for j in pre[i]:
-            if o["k"] == "x" or j in o.get("after", ()) or (o["q"] == "t" and ops[j]["q"] == "t"):
+            if o["k"] == "x" or (o["q"] == "t" and ops[j]["q"] == "t"):
                 continue
             if ops[j]["k"] == "c":
                 q = ops[j]["q"]
@@ -187,7 +297,7 @@ def rank_program(g, core, T, topo):
     rank = T.rank_of(core)
     if rank is None:
         return
-    ops, sends, tag = [], [], ["a"]
+    ops, sends, lines = [], [], {}
 
     def v(n, a=None, b=None, st=1, p=None):
         if a is None:
@@ -204,25 +314,25 @@ def rank_program(g, core, T, topo):
         full = [x for x in outs + ins if isinstance(x, tuple)]
         wide = [SCRATCH[x[1][0][0]][2] in (F32, I32) for x in full if x[2] == full[0][2]]
         if k == "x":
-            return 0.0, TX
+            return 0.0, WAY
         if k == "r":
-            return 0.5, 0.0
+            return CALL, 0.0
         if k == "d":
             return 0.1, 2.0 + full[0][2] * (4 if wide[0] else 2) * 128 / 500e3
         n = outs[0][2]
         if q == "t":
             return max(64, n) * PE * (4 if SCRATCH[ins[1][1][0][0]][2] == F32 else 1), 0.0
         if q == "g":
-            return 0.2 + 2 * n * CY, 0.0
+            return 0.16 + 2 * n * CY, 0.0
         if len(outs[0]) == 5:
             return 0.06 + 3.8 * n * CY, 0.0
-        if len(ins[0]) == 5:
+        if len(ins) and len(ins[0]) == 5:
             return 0.07 + 1.56 * n * CY, 0.0
         if q == "s":
-            return max(64, n) * CY, 0.0
+            return 0.075 + n * CY, 0.0
         if two:
-            return max(64, n * (1 if any(SCRATCH[x[1][0][0]][0] == "psum" for x in ins) else 2)) * CY, 0.0
-        return max(64, n * (1 if any(wide) else 0.5)) * CY, 0.0
+            return 0.06 + n * (1 if any(SCRATCH[x[1][0][0]][0] == "psum" for x in ins) else 2) * CY, 0.0
+        return 0.06 + n * (1 if any(wide) else 0.5) * CY, 0.0
 
     def add(q, k, f, outs, ins, two=False, **kw):
         r, w = [], []
@@ -237,16 +347,22 @@ def rank_program(g, core, T, topo):
                 w += x[1]
         c, l = span(q, k, outs, ins, two)
         m = "sc" if outs and len(outs[0]) == 5 else "ga" if ins and len(ins[0]) == 5 else ""
-        o = {"q": q, "k": k, "f": f, "r": r, "w": w, "c": c, "l": l, "m": m,
-             "tag": q + (w[0][0] + tag[0] + str(w[0][1] // 1024 % 3) if w else tag[0])}
+        o = {"q": q, "k": k, "f": f, "r": r, "w": w, "c": c, "l": l, "m": m}
         o.update(kw)
         ops.append(o)
+
+    def line(name):
+        ops[-1]["after"] = lines.get(name, [])
+        lines[name] = [len(ops) - 1]
 
     def ap(x):
         return x[0] if isinstance(x, tuple) else x
 
     def cp(o, i):
         add("v", "c", lambda e: e.tensor_copy(o[0], i[0]), [o], [i])
+
+    def fill(o, c):
+        add("v", "c", lambda e: e.memset(o[0], c), [o], [])
 
     def tt(o, a, b, op):
         add("v", "c", lambda e: e.tensor_tensor(o[0], a[0], b[0], op), [o], [a, b], True)
@@ -278,6 +394,17 @@ def rank_program(g, core, T, topo):
     def mm(o, l, r, start, stop):
         add("t", "c", lambda e: e.matmul(o[0], l[0], r[0], start, stop), [o], [l, r])
 
+    def mms(o, pairs, start=True, stop=True):
+        for j, (l, r) in enumerate(pairs):
+            mm(o, l, r, start and j == 0, stop and j == len(pairs) - 1)
+
+    def mmg(o, pairs, start=True, stop=True):
+        def f(e):
+            return [e.matmul(o[0], l[0], r[0], start and j == 0, stop and j == len(pairs) - 1)
+                    for j, (l, r) in enumerate(pairs)][-1]
+        add("t", "c", f, [o], [x for p in pairs for x in p])
+        ops[-1]["c"] = sum(span("t", "c", [o], list(p), False)[0] for p in pairs)
+
     def iota(o, pat, base, ch, small=True):
         if small:
             add("g", "c", lambda e: e.iota(o[0], pat, base, ch, allow_small_or_imprecise_dtypes=True), [o], [])
@@ -287,14 +414,17 @@ def rank_program(g, core, T, topo):
     def gfill(o, c):
         iota(o, [[0, o[1][0][2] - o[1][0][1]]], c, 0)
 
-    def asel(o, i, pat, base, ch, op, fill):
-        add("g", "c", lambda e: e.affine_select(o[0], i[0], pat, op, fill, base, ch), [o], [i])
+    def asel(o, i, pat, base, ch, op, fl):
+        add("g", "c", lambda e: e.affine_select(o[0], i[0], pat, op, fl, base, ch), [o], [i])
 
-    def load(q, o, src, part=None):
-        if part is not None:
-            n, a, b = o[1][0]
-            o = (o[0], [(n, a + part, a + part + 1)], o[2])
+    def part(o, x):
+        n, a, b = o[1][0]
+        return (o[0], [(n, a + x, a + x + 1)], o[2])
+
+    def load(q, o, src, x=None):
+        o = o if x is None else part(o, x)
         add(q, "d", lambda e: e.dma_start(o[0], src), [o], [])
+        line("load" + q)
 
     def store(q, dst, i):
         add(q, "d", lambda e: e.dma_start(dst, i[0]), [], [i])
@@ -302,41 +432,54 @@ def rank_program(g, core, T, topo):
     def dcopy(q, o, i):
         add(q, "d", lambda e: e.dma_start(o[0], i[0]), [o], [i])
 
-    def send(x, sign, sn, s0, dn, d0, d1=1, d2=N, k=1):
-        sem = "arr%d" % x
-        tr, used = [], []
-        for d in range(d1, d2):
-            dst = T.cores[(rank + sign * d) % N]
-            rid, pid = topo.addr(dst, core)
-            en = [e for e in topo.engines(core, dst) if e not in used][:k]
-            used += en
-            tr.append(RemoteDMATransfer(
-                dst_ids=[DstId(rid=rid, pnc=pid)], dma_engine_mask=sum(1 << e for e in en), remote_sem=T.sem[sem],
-                src=T[sn][:, s0 + (d - 1) * G:s0 + d * G], dst=T[dn][:, d0 + (d - 1) * G:d0 + d * G]))
-        n = (d2 - d1) * k
-        add("g", "r", lambda e: e.remote_dma_fused(tr, local_sem=T.sem["sent"]), [], [v(sn, s0, s0 + GW)], n=n)
-        ops[-1]["after"] = sends[-1:]
-        sends.append(len(ops) - 1)
-        add("x", "x", None, [v(dn, d0 + (d1 - 1) * G, d0 + (d2 - 1) * G)], [], sem=sem, n=n)
-        if k > 1 and d1 == 1:
-            ops[-1]["l"] = TX - 1.0
+    def send(calls, sign, sn, s0, dn, d0, ahead=0):
+        for x, (d1, d2, k) in enumerate(calls):
+            sem, tr, used = "arr%d" % len(sends), [], []
+            for d in range(d1, d2):
+                dst = T.cores[(rank + sign * d) % N]
+                rid, pid = topo.addr(dst, core)
+                en = [e for e in topo.engines(core, dst) if e not in used][:k]
+                used += en
+                tr.append(RemoteDMATransfer(
+                    dst_ids=[DstId(rid=rid, pnc=pid)], dma_engine_mask=sum(1 << e for e in en), remote_sem=T.sem[sem],
+                    src=T[sn][:, s0 + (d - 1) * G:s0 + d * G], dst=T[dn][:, d0 + (d - 1) * G:d0 + d * G]))
+            n = (d2 - d1) * k
+            add("g", "r", lambda e, tr=tr: e.remote_dma_fused(tr, local_sem=T.sem["sent"]), [],
+                [v(sn, s0 + (d1 - 1) * G, s0 + (d2 - 1) * G)], n=n)
+            line("send")
+            if not sends:
+                ops[-1]["c"] += 2.0
+            sends.append(len(ops) - 1)
+            add("x", "x", None, [v(dn, d0 + (d1 - 1) * G, d0 + (d2 - 1) * G)], [], sem=sem, n=n)
+            ahead += 128 // k
+            ops[-1]["l"] += ROW * ahead - CALL * x
 
-    def cmat(i, k=128):
-        return v("cm", i * 128, (i + 1) * 128, p=(0, k))
+    def cmat(i, p=None):
+        return v("cm", i * 128, (i + 1) * 128, p=p)
+
+    def fmat(i, p=None):
+        return v("cf", i * 128, (i + 1) * 128, p=p)
 
     def sel(x):
         return v("sel", x * 128, (x + 1) * 128)
 
-    h = (0, 64)
+    def picks(s, n, a, b):
+        return [(sel(s + k), v(n, a + k, b, 16)) for k in range(16)]
 
-    def spread(o, s, a, b, start=True, stop=True):
-        mm(o, v("ex", s * 128, (s + 1) * 128, p=h), v("m8h", a, b, p=h), start, stop)
+    def col(i, p=None):
+        return v("pcf", i, i + 1, p=p)
 
-    P16 = v("pcf", 0, 1)
+    h, hb, hk = (0, 64), (32, 64), (64, 72)
+
+    def spread(s, a, b):
+        p, e = (hk, XB) if s == XK else (h, s)
+        return (v("ex", e * 128, (e + 1) * 128, p=p), v("m8h", a, b, p=p))
+
     BET = v("bet", 0, 1)
 
-    load("y", v("t64", 0, 128, p=h), T.ti[:])
-    load("s", v("t64", 128, 256, p=h), T.kd[:])
+    for x in range(2):
+        load("y", v("t128", p=(64 * x, 64 * x + 32)), T.ti[:, 512 * x:512 * x + 512], x)
+        load("s", v("t128", p=(64 * x + 32, 64 * x + 64)), T.kd[:, 512 * x:512 * x + 512], 2 + x)
     load("y", v("sni", p=(16, 128)), T.snd[0:112, :], 0)
     load("s", v("sni", p=(0, 16)), T.snd[112:128, :], 1)
     load("y", v("ash", p=(16, 128)), T.a0[0:112, :], 0)
@@ -344,342 +487,400 @@ def rank_program(g, core, T, topo):
     load("y", v("cai"), T.ca[:])
     load("s", BET, T.be[:])
     for s, src in ((XT, T.ti[:, 0:384]), (XK, T.kd[:, 0:384]), (XU0, T.us[:, 0:384]), (XU1, T.us[:, 384:768]),
-                   (XC, T.cl[:]), (XL0, T.lp[:, 0:384]), (XL1, T.lp[:, 384:768]), (XL2, T.lp[:, 640:1024])):
+                   (XC, T.cl[:]), (XL0, T.lp[:, 0:384]), (XL1, T.lp[:, 384:768]), (XL2, T.lp[:, 640:1024]),
+                   (XB, T.bg[:])):
         load("y", v("m8", p=(8 * s, 8 * s + 8)), src, s)
-    load("y", v("kw", 16, 2064), T.k0[:])
-    load("y", v("mb", p=(0, 8)), T.bg[:])
-    load("y", v("aw", 0, E), T.a0[:])
+    load("y", v("kw", SP, KWID), T.k0[:])
+    load("y", v("aw", 16, 16 + E), T.a0[:])
 
-    iota(v("pci", 0, 1), [[0, 1]], 0, 1, False)
-    iota(v("ji", 0, 128), [[1, 128]], 128, -2, False)
-    iota(v("mk8", 8, 16), [[2, 8]], 0, 0)
+    iota(v("pci", 0, 2), [[1, 2]], 0, 1, False)
+    iota(v("ji", 0, 128), [[1, 128]], 512, -4, False)
+    iota(v("mk4", 4, 8), [[4, 4]], 0, 0)
     iota(v("mc"), [[0, 8], [1, 16]], 0, 0)
     asel(v("mc"), v("mc"), [[-16, 8], [0, 16]], 0, 1, OP.is_ge, -2.0)
     asel(v("mc"), v("mc"), [[16, 8], [0, 16]], 15, -1, OP.is_ge, -2.0)
-    iota(v("exv", p=h), [[-1, 8], [0, 16]], 0, 1)
+    iota(v("exv", 0, 128), [[-1, 8], [0, 16]], 0, 1)
+    asel(v("exv", 128, 256), v("exv", 0, 128), [[0, 8], [1, 16]], -2, 0, OP.is_ge, -99.0)
     iota(v("r16"), [[0, 12], [1, 16]], 0, 0)
-    iota(v("ty", 0, 33), [[1, 33]], 0, 0)
-    iota(v("wc", 16, 28), [[-16, 12]], 95, 0)
-    iota(v("dum", 64, 76), [[16, 12]], 0, 0)
-    iota(v("thr", M, 2 * M), [[-1, M]], 95, 0)
+    iota(v("d12", 0, 12), [[-16, 12]], 176 - SP + 1, 0)
 
-    ts(v("pci", 1, 2), v("pci", 0, 1), 15, OP.bitwise_and)
-    ts(v("pci", 2, 3), v("pci", 0, 1), 14, OP.bitwise_and)
-    cp(v("pcf", 0, 2), v("pci", 1, 3))
+    ts(v("pci", 2, 4), v("pci", 0, 2), 15, OP.bitwise_and)
+    for j, c in ((4, 12), (5, 3), (6, 1)):
+        ts(v("pci", j, j + 1), v("pci", 0, 1), c, OP.bitwise_and)
+    cp(v("pcf", 0, 5), v("pci", 2, 7))
     ts(v("ji", 128, 256), v("ji", 0, 128), 127, OP.bitwise_and)
-    for i, c in ((E0, 16), (E1, 17), (U0, 0), (U1, 1)):
-        ts(cmat(i), v("ji", 128, 256), float(c), OP.is_equal)
-    ts(v("mk8", 0, 8), v("mk8", 8, 16), v("pcf", 1, 2), OP.is_equal)
-    for x in range(8):
-        ts(sel(x), v("mc"), float(x), OP.is_equal)
+    for c, a, b in ((EAT, 16.0, 18.0), (EBY, 1.0, 0.125)):
+        fill(col(c), a)
+        fill(col(c, (32, 64)), b)
+        fill(col(c, (96, 128)), b)
+    ts(cmat(EM), v("ji", 128, 256), col(EAT), OP.is_equal, col(EBY), OP.mult)
+    ts(cmat(EL), v("ji", 128, 256), 17.0, OP.is_equal)
+    ts(v("mk4", 0, 4), v("mk4", 4, 8), col(P12), OP.is_equal)
+    ts(col(KC8), col(P3), 2.0, OP.is_equal, 8.0, OP.mult)
+    act(col(K18), col(KC8), AF.Identity, 0.0, 1.0 / 64)
 
-    ts(v("t64", 256, 384, p=h), v("t64", 0, 128, p=h), 8.0, OP.mult)
+    cp(v("hl", 0, 128), v("t128"))
     cp(v("snu"), v("sni"))
-    tt(v("t64", 0, 128, p=h), v("t64", 256, 384, p=h), v("t64", 128, 256, p=h), OP.add)
-    ts(v("t64", 384, 512, p=h), v("t64", 0, 128, p=h), 63, OP.bitwise_and)
-    cp(v("h64", 128, 256, p=h), v("t64", 384, 512, p=h))
-    tt(v("h64", 0, 128, p=h), v("t64", 0, 128, p=h), v("t64", 384, 512, p=h), OP.subtract)
-
-    def digits(a, b, bankn, dst):
-        mm(v(bankn, 0, 128), cmat(a, 64), v("h64", 0, 128, p=h), True, False)
-        mm(v(bankn, 0, 128), cmat(b, 64), v("h64", 128, 256, p=h), False, True)
-        cp(v("dg"), v(bankn, 0, 128))
-        for x in range(8):
-            ts(v(dst, 128 * x, 128 * x + 128), v("dg"), v("mk8", x, x + 1), OP.mult)
-
+    tt(v("hl", 128, 256), v("t128"), v("hl", 0, 128), OP.subtract)
+    for x in range(2):
+        a = (64 * x, 64 * x + 64)
+        mms(v("p%d" % x, 0, 128), ((cmat(EM, a), v("hl", 0, 128, p=a)), (cmat(EL, a), v("hl", 128, 256, p=a))))
+    ts(v("dg", 0, 128), v("p0", 0, 128), col(K18), OP.add)
+    act(v("dg", 128, 256), v("p1", 0, 128), AF.Identity, col(K18))
+    for x in range(8):
+        o, i = v("tks", 128 * x, 128 * x + 128), v("dg", 128 * (x // 4), 128 * (x // 4) + 128)
+        if x < 6:
+            ts(o, i, v("mk4", x % 4, x % 4 + 1), OP.mult)
+        else:
+            act(o, i, AF.Identity, 0.0, v("mk4", x % 4, x % 4 + 1))
     act(v("fb", GW, 2 * GW), ind(v("ash"), v("snu")), AF.Copy)
-    digits(E0, E1, "p0", "tks")
     cp(v("fb", 0, 448), ind(v("tks"), v("snu", 0, 28)))
     act(v("fb", 448, GW), ind(v("tks"), v("snu", 28, 56)), AF.Copy)
-    send(0, 1, "fb", 0, "tkw", E)
-    send(1, 1, "fb", GW, "aw", E)
+    slots = [len(ops) - 2, len(ops) - 1]
+    send(WHOLE, 1, "fb", 0, "tkw", 16 + E)
+    send(WHOLE, 1, "fb", GW, "aw", 16 + E, 100)
+    dcopy("y", v("tkw", 16, 16 + E, p=(0, 112)), v("tks", p=(16, 128)))
+    ops[-1]["w"] = [("tkw", 17, 16 + E)]
+    dcopy("y", part(v("tkw", 16, 16 + E, p=(112, 128)), 0), v("tks", p=(0, 16)))
 
-    digits(U0, U1, "p1", "tkw")
-    cp(v("cu"), v("cai"))
-    for x in range(8, 16):
+    ts(v("cu"), v("cai"), 16.0, OP.add)
+    ops[-1]["after"] = slots
+    for x in range(16):
         ts(sel(x), v("mc"), float(x), OP.is_equal)
-    cp(v("m8h", p=h), v("m8", p=h))
-    for s in range(8):
-        ts(v("ex", s * 128, (s + 1) * 128, p=h), v("exv", p=h), float(8 * s), OP.is_equal,
-           -8.0 if s == XT else 1.0, OP.mult)
-    ts(v("ex32", p=(0, 8)), v("exv", p=(0, 8)), 0.0, OP.is_equal)
-    cp(v("mbf", p=(0, 8)), v("mb", p=(0, 8)))
-    ts(v("c1"), v("cai"), 1.0, OP.add)
+    fill(v("pcf", MMUL, MMUL + 2), 1.0)
+    fill(col(MADD, (0, 32)), 0.0)
+    fill(col(MMUL, (64, 128)), 8.0)
+    fill(col(MADD, (64, 128)), -10240.0)
+    ts(v("m8h", p=(0, 72)), v("m8", p=(0, 72)), col(MMUL, (0, 72)), OP.mult, col(MADD, (0, 72)), OP.add)
+    ops[-1]["after"] = slots
+    cp(v("mbf", p=hb), v("m8", p=hb))
+    ops[-1]["after"] = slots
+    for s in range(7):
+        e0 = 128 if s >= XL0 else 0
+        ts(v("ex", s * 128, (s + 1) * 128, p=h), v("exv", e0, e0 + 128, p=h), float(8 * s), OP.is_equal,
+           -1.0 if s == XT else 1.0, OP.mult)
+    ts(v("ex", XB * 128, (XB + 1) * 128, p=hk), v("exv", 0, 128, p=hk), 64.0, OP.is_equal)
+    ts(fmat(XBM, hb), v("exv", 0, 128, p=hb), 56.0, OP.is_equal, 1.0 / 16, OP.mult)
+    ts(v("c1"), v("cu"), -15.0, OP.add)
     ts(cmat(ONES), v("mc"), 0.0, OP.is_ge)
-    ts(cmat(TRI), v("mc"), P16, OP.is_ge, 256.0, OP.mult)
-    ts(cmat(R15), v("mc"), 0.0, OP.is_ge, -1.0, OP.mult)
-    ts(v("m8h", p=(8 * XK, 8 * XK + 8)), v("m8h", p=(8 * XK, 8 * XK + 8)), 8.0, OP.mult, 1.0, OP.add)
-    spread(v("p5", 0, 384), XU0, 0, 384)
-    spread(v("p6", 0, 384), XU1, 0, 384)
-    spread(v("p4", 0, 384), XC, 0, 384)
+    ts(cmat(NON), v("mc"), 0.0, OP.is_ge, -1.0, OP.mult)
+    act(fmat(NON32), cmat(NON), AF.Copy)
+    ts(cmat(TRI), v("mc"), col(P16), OP.is_ge, 256.0, OP.mult)
+    ts(col(TCOL), col(P3), 2.0, OP.is_lt)
+    ts(col(LT4), col(P16), 4.0, OP.is_lt)
+    ts(col(C15), col(P16), 15.0, OP.is_equal, -BIG, OP.mult)
+    ts(col(NDZ), col(P16), 0.0, OP.not_equal, -1.0, OP.mult)
+    act(col(NPAR), col(P1), AF.Identity, 0.0, -1.0)
+    act(col(SGN), col(P1), AF.Identity, 1.0, -2.0)
+    act(col(VALC), col(LT4), AF.Identity, 0.0, col(SGN))
+    act(col(DCON), col(NDZ), AF.Identity, 0.0, -1024.0)
+    act(col(PQ), col(P16), AF.Identity, 0.0, 1.0 / 16)
+    act(col(TB), col(P16), AF.Identity, -128.0, -256.0)
+    act(cmat(TRS), v("mc"), AF.Sigmoid, col(TB), 256.0)
+    ops[-1]["c"] += 1.3
+    ops[-1]["r"] += v("fb", 0, 2 * GW)[1]
+    line("step")
+    ts(cmat(ID), v("mc"), col(P16), OP.is_equal)
+    for o, c in ((cmat(NI), -1.0), (cmat(ID64), 64.0), (fmat(ID32), 1.0), (cmat(DLD), col(NDZ))):
+        act(o, cmat(ID), AF.Identity, 0.0, c)
+    ts(cmat(DLP), v("mc"), col(NXT), OP.is_equal)
+    ts(cmat(ELM), v("mc"), 2.0, OP.is_ge, col(C15), OP.mult)
+    for i, c in ((VALM, VALC), (UT, TCOL), (KK, KC8)):
+        act(cmat(i), cmat(ONES), AF.Identity, 0.0, col(c))
+    act(cmat(UPM), cmat(VALM), AF.Relu)
+    for x in range(16):
+        if x < 8:
+            asel(sel(16 + x), cmat(KK), [[0, 8], [1, 16]], -x, 0, OP.is_equal, 0.0)
+            ops[-1]["after"] = sends[-1:]
+        else:
+            ts(sel(16 + x), v("mc"), float(x), OP.is_equal, col(KC8), OP.mult)
+    for b, s in (("p5", XU0), ("p6", XU1), ("p4", XC)):
+        mms(v(b, 0, 384), (spread(s, 0, 384),))
     act(v("urep", 0, 384), v("p5", 0, 384), AF.Copy)
     act(v("urep", 384, 768), v("p6", 0, 384), AF.Copy)
-    ts(v("oh"), v("p4", 0, 384), P16, OP.is_equal)
+    ts(v("oh"), v("p4", 0, 384), col(P16), OP.is_equal)
+    mms(v("p7", 0, 384), ((fmat(XBM, hb), v("mbf", p=hb)),))
+    for x in range(2):
+        tt(v("ub", 384 * x, 384 * x + 384), v("p7", 0, 384), v("urep", 384 * x, 384 * x + 384), OP.mult)
     act(v("oh7"), v("oh"), AF.Identity, 7.0, -1.0)
-    spread(v("p5", 0, 384), XL0, 0, 384)
-    spread(v("p6", 0, 384), XL1, 0, 384)
-    spread(v("p4", 0, 256), XL2, 128, 384)
-    act(v("lw", 8, 392), v("p5", 0, 384), AF.Identity, 1.0)
-    act(v("lw", 392, 776), v("p6", 0, 384), AF.Identity, 1.0)
-    act(v("lw", 776, E + 8), v("p4", 0, 256), AF.Identity, 1.0)
-    ln2 = math.log(2.0)
-    ts(v("wc", 32, 44), v("wc", 16, 28), P16, OP.subtract)
-    act(v("wc", 0, 12), v("wc", 32, 44), AF.Exp, 0.0, ln2)
-    ops[-1]["c"] += 1.5
-    ops[-1]["r"] += v("fb", 0, 2 * GW)[1] + v("thr", M, 2 * M)[1]
-    ops[-1]["w"] += v("thr", 2 * M - 1, 2 * M)[1]
-    act(v("thr", M, 2 * M), v("thr", M, 2 * M), AF.Exp, 0.0, ln2)
-    ts(v("th"), v("r16"), P16, OP.is_equal, 2.5, OP.mult)
-    ts(v("rst"), v("r16"), 0.0, OP.not_equal)
+    ts(v("mkc"), v("r16"), col(P16), OP.not_equal, -BIG, OP.mult)
     ts(v("big"), v("r16"), 0.0, OP.is_equal, 1.0e6, OP.mult)
-    for a, c in ((0, 16 + W), (16, 2064), (32, 1 + W), (48, 2049)):
-        ts(v("dum", a, a + 12), v("dum", 64, 76), P16, OP.add, float(c), OP.add)
-    ts(v("pcf", 2, 3), P16, 0.0, OP.is_equal, -5000.0, OP.mult)
-    tt(v("thr", 0, M), v("thr", M, 2 * M), v("th"), OP.mult)
+    gfill(v("d0"), int(BIG))
+    ts(v("d0", 0, M, 16), v("d12", 0, 12), col(P16), OP.add)
     row = [[-1, 128]]
-    asel(cmat(DM), cmat(R15), row, -1, 1, OP.is_equal, 0.0)
-    asel(cmat(DM), cmat(DM), row, 0, 1, OP.not_equal, 1.0)
-    asel(cmat(DL), cmat(ONES), row, 1, 1, OP.is_equal, 0.0)
-    asel(cmat(DL), cmat(DL), row, 0, 1, OP.not_equal, -1.0)
-    asel(cmat(DU), cmat(R15), row, 0, 1, OP.is_gt, 0.0)
-    asel(cmat(DU), cmat(DU), row, 0, 1, OP.not_equal, 1.0)
-    asel(cmat(R15), cmat(R15), [[-16, 8], [0, 16]], -15, 1, OP.is_equal, 0.0)
-    gfill(v("ty", 232, 463), 0)
-    gfill(v("ty", 464, 695), 1)
-    gfill(v("hi", 0, 64), 0)
-    gfill(v("kw", 0, 16), 0)
-    gfill(v("kw", 2064, KWID), 0)
-    gfill(v("zb", 0, RW), 0)
-    gfill(v("cm", NI * 128, (NUSH + 1) * 128), 0)
-    for i, bases in ((NI, (0,)), (NSH, (16, -112)), (NUSH, (-16, 112))):
+    iota(v("ty", 0, 17), [[1, 17]], 0, 0)
+    for o, c in [(v("ty", 120, 239), 0), (v("ty", 240, 359), 1), (v("hi", 0, 128), 0), (v("tkw", 0, 16), 0),
+                 (v("aw", 0, 16), 0), (v("kw", 0, SP), 0)]:
+        gfill(o, c)
+    for i, op, b in ((DM, OP.is_equal, -1), (DU, OP.is_gt, 0)):
+        asel(cmat(i), cmat(NON), row, b, 1, op, 0.0)
+        ops[-1]["after"] = sends[-1:]
+        asel(cmat(i), cmat(i), row, 0, 1, OP.not_equal, 1.0)
+    for o in ([v("zb", a, a + 532) for a in range(3 * RW, PL, 532)] + [v("aw", t * AW, t * AW + 16) for t in range(1, R)]
+              + [v("lw", 0, 8), v("lw", E + 8, E + 16), v("cm", NSH * 128, (NUSH + 1) * 128)]):
+        gfill(o, 0)
+    for i, bases in ((NSH, (16, -112)), (NUSH, (-16, 112))):
         for b in bases:
             asel(cmat(i), cmat(i), row, b, 1, OP.not_equal, -1.0)
-    gfill(v("lw", 0, 8), 0)
-    gfill(v("lw", E + 8, E + 16), 0)
+    for p, s, a, b, c in (("p5", XL0, 0, 384, 8), ("p6", XL1, 0, 384, 392), ("p3", XL2, 128, 384, 776)):
+        mms(v(p, 0, b - a), (spread(s, a, b),))
+        act(v("lw", c, c + b - a), v(p, 0, b - a), AF.Relu, col(NPAR))
 
     def ratio_table():
         for n in range(1, 7):
-            ts(v("ty", 232 + n, 463, 7), v("ty", 0, 33), BET, OP.mult, -1.0 / (7 - n), OP.mult)
-        scan(v("ty", 696, 927), v("ty", 232, 463), v("ty", 464, 695), 0.0, OP.mult, OP.add)
-        ts(v("hi", 64, 128), v("hi", 0, 64), v("ty", 926, 927), OP.add)
-        scan(v("hi", 128, 161), v("hi", 64, 97), v("hi", 0, 33), 1.0, OP.mult, OP.add)
-        recip(v("hi", 176, 177), v("hi", 160, 161))
-        scan(v("hi", 192, 256), v("hi", 64, 128), v("hi", 0, 64), v("hi", 176, 177), OP.mult, OP.add)
-
-    def ratio_fill():
-        for b in range(32):
-            act(v("rt", b, 2048, 32), v("hi", 192, 256), AF.Identity, 0.0, v("ty", 702 + 7 * b, 703 + 7 * b))
+            ts(v("ty", 120 + n, 239, 7), v("ty", 0, 17), BET, OP.mult, -1.0 / (7 - n), OP.mult)
+            ops[-1]["w"] = [("ty", 120 + n, 121 + n)]
+            ops[-1]["after"] = slots
+        scan(v("ty", 360, 479), v("ty", 120, 239), v("ty", 240, 359), 0.0, OP.mult, OP.add)
+        ts(v("hi", 128, 256), v("hi", 0, 128), v("ty", 478, 479), OP.add)
+        scan(v("hi", 256, 321), v("hi", 128, 193), v("hi", 0, 65), 1.0, OP.mult, OP.add)
+        recip(v("hi", 336, 337), v("hi", 320, 321))
+        scan(v("hi", 384, 512), v("hi", 128, 256), v("hi", 0, 128), v("hi", 336, 337), OP.mult, OP.add)
+        for b in range(16):
+            act(v("rt", b, 2048, 16), v("hi", 384, 512), AF.Identity, 0.0, v("ty", 366 + 7 * b, 367 + 7 * b))
             ops[-1]["w"] = [("rt", b, b + 1)]
-        act(v("rt", 0, 1), v("hi", 0, 1), AF.Copy)
+            line("step")
 
     def tk_gather(q, t, i0, i1):
-        lo = (t % 2) * M
-        move(q, v("tg", 16 * i0, 16 * i1), ind(v("tkw"), v("cu", lo + i0, lo + i1)))
+        move(q, v("tg", 16 * i0, 16 * i1), ind(v("tkw"), v("cu", t * M + i0, t * M + i1)))
 
-    def tk_extract(t, i0, i1):
-        lo = (t % 2) * M
-        o = v("p3", i0, i1)
-        spread(o, XT, lo + i0, lo + i1, True, False)
-        for k in range(16):
-            mm(o, sel(k), v("tg", 16 * i0 + k, 16 * i1, 16), False, k == 15)
+    def bins(t, i0, i1, bx, by):
+        lo = t * M
+        X, Y, a, q = v(bx, i0, i1), v(by, M + i0, M + i1), v("ab", i0, i1), v("qq", i0, i1)
+        for c in range(i0, i1, 64):
+            mmg(v(bx, c, c + 64), [spread(XT, lo + c, lo + c + 64)] + picks(0, "tg", 16 * c, 16 * c + 1024))
+        act(a, X, AF.Abs, -0.5625)
+        act(q, a, AF.Identity, 159.515625, 1.0 / 32)
+        mm(Y, *spread(XK, lo + i0, lo + i1), True, False)
+        for c in range(i0, i1, 64):
+            mmg(v(by, M + c, M + c + 64), picks(16, "tg", 16 * c, 16 * c + 1024), False, False)
+        mm(Y, cmat(ID64), q, False, True)
+        ts(v("binu", lo + i0, lo + i1), Y, -1.0, OP.add)
 
-    def bins(t):
-        lo = (t % 2) * M
-        X, Y = v("p3", 0, M), v("p3", M, 2 * M)
-        spread(Y, XK, lo, lo + M)
-        y = v("bf", 3 * M, 4 * M)
-        a, b, kc, li = [v("bi", j * M, (j + 1) * M) for j in range(4)]
-        xi, b1 = v("xi", lo, lo + M), v("b1", t * M, (t + 1) * M)
-        if t == 0:
-            ts(y, X, -1.0, OP.mult, 7.0, OP.add)
-        else:
-            act(y, X, AF.Identity, 7.0, -1.0)
-        cp(xi, X)
-        tt(a, X, y, OP.max)
-        ts(kc, xi, 7, OP.bitwise_and)
-        ts(b, a, 2, OP.arith_shift_right, 1984, OP.bitwise_and)
-        tt(Y, kc, Y, OP.add)
-        ts(li, a, 3, OP.arith_shift_right)
-        tt(b1, b, Y, OP.add)
-        cp(v("l16"), li)
-        ts(v("binu", t * M, (t + 1) * M), b1, -1.0, OP.add)
-        mm(Y, cmat(DL), v("l16"), True, True)
-        mm(X, cmat(R15), v("l16"), True, True)
+    def lags(t, by):
+        cp(v("b1", t * M, (t + 1) * M), v(by, M, 2 * M))
+        ts(v("l16"), v("ab"), 1024.0, OP.add)
+        mms(v("p3", 0, M), [(cmat(i), v("l16")) for i in (DLP, DLD)])
+        ts(v("dlt", t * M, (t + 1) * M), v("p3", 0, M), col(DCON), OP.add)
 
     def steps(t):
         lo = (t % 2) * M
-        mm(v("p7", 0, M), cmat(DM), v("c1", lo, lo + M), True, True)
-        mm(v("p7", M, 2 * M), cmat(DM), v("b1", t * M, (t + 1) * M), True, True)
+        mms(v("p7", 0, M), [(cmat(DM), v(n, lo, lo + M)) for n in (("c1",) if t < 2 else ("c1", "tc"))])
+        if t < R - 1:
+            mms(v("p7", M, 2 * M), [(cmat(DM), v("b1", lo, lo + M))] + [(cmat(DM), v("tb"))] * (t // 2))
 
-    def lags(t):
-        ts(v("dlt", t * M, (t + 1) * M), v("p3", M, 2 * M), v("pcf", 2, 3), OP.add, 1024.0, OP.add)
-        act(v("e15", t * M, (t + 1) * M), v("p3", 0, M), AF.Exp, 0.0, BET)
+    def elected(t, j, i0, i1):
+        s = 2 if j else t % 2
+        a, b = s * M + i0, s * M + i1
+        tt(v("hd", a, b), v("p7", j * M + i0, j * M + i1), v("hit", (t % 2) * M + i0, (t % 2) * M + i1), OP.mult)
+        mm(v("p0", i0, i1), cmat(ONES), v("hd", a, b), True, True)
+        cp(v("rep", j * M + i0, j * M + i1), v("p0", i0, i1))
+        li = v("p1" if i0 == 0 else "p2", 256 + i0, 256 + i1)
+        mms(li, [(cmat(ID), v("mkc", i0, i1)), (cmat(ONES), v("hd", a, b))])
+        scan(v("lst", a, b), v("d0", i0, i1), li, BIG, OP.min, OP.max)
 
-    def k_gather(q, t, i0, i1):
-        move(q, v("kg", 16 * i0, 16 * i1), ind(v("kw", 16, 2064), v("binu", t * M + i0, t * M + i1)))
+    def weights(t, bank, i0, i1):
+        mmg(v(bank, 256 + i0, 256 + i1), picks(0, "pr", t * C + 16 * i0, t * C + 16 * i1)
+            + [(cmat(ID), v("wn", i0, i1))] * (t // 2))
 
-    def elected(j, s, i0, i1):
-        a, b = j * M + i0, j * M + i1
-        tt(v("hd", a, b), v("p7", a, b), v("th", i0, i1), OP.mult)
-        mm(v("p2", i0, i1), cmat(ONES), v("hd", a, b), True, True)
-        cp(v("rep", s * M + i0, s * M + i1), v("p2", i0, i1))
-        li = v("p1", 400 + i0 // 16, 400 + i1 // 16)
-        for x in range(16):
-            mm(li, sel(x), v("hd", a + x, b, 16), x == 0, x == 15)
-        cp(v("lst", 16 * s + i0 // 16, 16 * s + i1 // 16), li)
+    def elect(t, i0, i1, wb, db):
+        lo = (t % 2) * M
+        w, w32, wu, D = v(wb, 256 + i0, 256 + i1), v("w32", lo + i0, lo + i1), v("wu", i0, i1), v(db, i0, i1)
+        tt(wu, w, v("urep", t * M + i0, t * M + i1), OP.mult)
+        cp(v("w16", i0, i1), w)
+        mms(D, [(cmat(TRI), v("w16", i0, i1)), (fmat(NON32), wu)], False)
+        if t < 2:
+            act(w32, w, AF.Identity, col(PQ))
+        act(v("hit", lo + i0, lo + i1), D, AF.Sigmoid, -128.0, 256.0)
+        line("step")
+        elected(t, 0, i0, i1)
 
-    def elect(t, i0, i1, w, x):
-        w16 = v("w16", (t % 2) * M + i0, (t % 2) * M + i1)
-        cp(w16, w)
-        mm(x, cmat(ONES), w16, False, True)
-        mm(v("p1", i0, i1), cmat(TRI), w16, True, True)
-        tt(v("th", i0, i1), x, v("urep", t * M + i0, t * M + i1), OP.mult)
-        tt(v("th", i0, i1), v("p1", i0, i1), v("th", i0, i1), OP.is_gt)
-        elected(0, t % 2, i0, i1)
-
-    def first_of(j, s):
-        dum = 16 * j
-        lst = v("lst", 16 * s, 16 * s + 12)
-        if j == 1:
-            elected(1, s, 0, M)
+    def first_of(t, j):
+        s = 2 if j else t % 2
+        mms(v("p4", 0, M), [(cmat(ID), v("mkc")), (cmat(ONES), v("hd", s * M, (s + 1) * M))], True, False)
         for y in range(12):
-            z = v("zz", y * M + 16 * y, (y + 1) * M)
-            ts(z, v("rep", s * M + 16 * y, (s + 1) * M), v("lst", 16 * s + y, 16 * s + y + 1), OP.is_equal,
-               v("wc", y, y + 1), OP.mult)
-            mm(v("p4", 16 * y, M), cmat(ONES), z, y == 0, y == 11)
-        tt(v("sm", 0, 12), lst, v("dum", dum + 32, dum + 44), OP.subtract)
-        tt(v("fl", 0, M), v("p4", 0, M), v("thr", 0, M), OP.is_lt)
-        scan(v("fl", M, 2 * M), v("rst"), v("fl", 0, M), 0.0, OP.mult, OP.add)
-        tt(v("sm", 16, 28), v("fl", M + 15, 2 * M, 16), v("sm", 0, 12), OP.mult)
-        tt(v("sm", 32, 44), v("sm", 16, 28), v("dum", dum, dum + 12), OP.add)
-        cp(v("offs", 16 * j, 16 * j + 12), v("sm", 32, 44))
+            z0, z1 = y * M + 16 * y, (y + 1) * M
+            ts(v("zz", z0, z1), v("rep", j * M + 16 * y, (j + 1) * M),
+               v("lst", s * M + 16 * y + 15, s * M + 16 * y + 16), OP.is_equal, -BIG, OP.mult)
+            if y < 11:
+                mm(v("p4", 16 * y + 16, M), cmat(ONES), v("zz", z0 + 16, z1), False, False)
+            mm(v("p4", 16 * y, 16 * y + 16), cmat(TRS), v("zz", z0, z0 + 16), False, y == 11)
+        scan(v("sc"), v("d0"), v("p4", 0, M), BIG, OP.min, OP.max)
+        ts(v("offs", 16 * j, 16 * j + 12), v("sc", 15, M, 16), SP - 1.0, OP.add)
 
     def ratios(t, c):
-        a = (t % 2) * C + 1024 * c
-        act(v("rg", a, a + 1024), ind(v("rt"), v("dlt", t * M + 64 * c, t * M + 64 * c + 64)), AF.Copy)
+        a, e = t * C + 1024 * c, t * M + 64 * c
+        for b in range(2):
+            act(v("rg", a + 512 * b, a + 512 * b + 512), ind(v("rt"), v("dlt", e + 32 * b, e + 32 * b + 32)), AF.Copy)
+        act(v("e15", e, e + 64), v("rg", a, a + 1024, 16), AF.Copy)
+        act(v("rg", a, a + 1024, 16), v("e15", e, e + 64), AF.Identity, 0.0, 0.0)
 
     def lam(t, c):
         a, so = 1024 * c, 1024 * ((3 * t + c) % 2)
-        o0 = t * M + 64 * c
+        lo, y = (t % 2) * M, v("ylf", t * M, (t + 1) * M)
         for b in range(0, 1024, LW):
-            scan(v("so", so + b, so + b + LW), v("rg", (t % 2) * C + a + b, (t % 2) * C + a + b + LW),
+            scan(v("so", so + b, so + b + LW), v("rg", 16 * lo + a + b, 16 * lo + a + b + LW),
                  v("pr", t * C + a + b, t * C + a + b + LW), 0.0, OP.mult, OP.add)
-        tt(v("ylf", o0, o0 + 64), v("so", so + 15, so + 1024, 16), v("e15", o0, o0 + 64), OP.mult)
+        tt(v("ylf", t * M + 64 * c, t * M + 64 * c + 64), v("so", so + 15, so + 1024, 16),
+           v("e15", lo + 64 * c, lo + 64 * c + 64), OP.mult)
         if c == 2:
-            store("y", T.yl[:, t * M:(t + 1) * M], v("ylf", t * M, (t + 1) * M))
-
-    def least(t):
-        f0, f1, f2 = [v("bf", j * M, (j + 1) * M) for j in range(3)]
-        ts(f0, v("w16", t * M, (t + 1) * M), 16.0, OP.mult, P16, OP.add)
-        vtr(f1, f0)
-        scan(f2, v("big"), f1, 0.0, OP.add, OP.min)
-        vtr(v("p3", 0, M), f2)
-        tt(v("rec"), f0, v("p3", 0, M), OP.is_equal)
+            if t >= 2:
+                new = v("en", lo, lo + M)
+                tt(new, new, v("pn", lo, lo + M), OP.mult)
+                tt(y, y, new, OP.add)
+            store("y", T.yl[:, t * M:(t + 1) * M], y)
 
     def candidates(t):
         lo = t * M
-        up, flag = v("up"), v("bf", 4 * M, 5 * M)
-        X, y, xi = v("p3", 0, M), v("p3", M, 2 * M), v("xi", lo, lo + M)
-        rep, lw, c1 = v("rep", lo, lo + M), v("lw", 8 + lo, 8 + lo + M), v("c1", lo, lo + M)
-        ts(y, rep, 0.0, OP.is_equal)
-        ts(v("offs", 32, 44), v("lst", 16 * t, 16 * t + 12), 1025.0, OP.min, 7.0, OP.add)
-        tt(y, y, lw, OP.mult)
-        tt(lw, y, rep, OP.add)
-        cp(up, ind(v("lw"), v("offs", 32, 44)))
-        mm(y, cmat(DU), v("rec"), True, True)
-        for k in range(16):
-            mm(v("p3", 400, 412), sel(k), v("up", k, M, 16), k == 0, k == 15)
-        ts(v("offs", 48, 60), v("p3", 400, 412), 0.0625, OP.mult, -1.0, OP.add)
-        tt(y, y, up, OP.min)
-        ts(flag, y, 0.0, OP.max)
-        tt(y, up, c1, OP.subtract)
-        tt(y, y, flag, OP.mult)
-        tt(c1, y, c1, OP.add)
-        act(v("tg", 0, M), ind(v("tkw"), v("offs", 48, 60)), AF.Copy)
-        spread(X, XT, lo, lo + M, True, False)
-        mm(X, cmat(ONES), v("tg", 0, M), False, True)
-        ts(v("cu", lo, lo + M), c1, -1.0, OP.add)
-        tt(X, X, xi, OP.subtract)
-        tt(X, X, flag, OP.mult)
-        tt(X, X, xi, OP.add)
-        bins(t + 2)
-        lags(t + 2)
+        X, Y, Z = v("p3", 0, M), v("p3", M, 2 * M), v("p3", 400, 412)
+        up, stay, tn = v("up"), v("flag", 2 * M, 3 * M), v("tn")
+        c1, b1, tc, flag = [v(n, lo, lo + M) for n in ("c1", "b1", "tc", "flag")]
+        new = v("offs", 48 + 16 * t, 60 + 16 * t)
+        f1, f2 = [v("bf", j * M, (j + 1) * M) for j in range(2)]
+        vtr(f1, v("w32", lo, lo + M))
+        scan(f2, v("big"), f1, 0.0, OP.add, OP.min)
+        vtr(X, f2)
+        tt(v("rec"), v("w32", lo, lo + M), X, OP.is_equal)
+        mms(Y, [spread(XL0, lo, lo + M), (cmat(ELM), v("hit", lo, lo + M)), (cmat(ONES), v("hd", lo, lo + M))])
+        act(v("lw", 8 + lo, 8 + lo + M), Y, AF.Relu, col(NPAR))
+        ts(v("offs", 32, 44), v("lst", lo + 15, lo + M, 16), 1025.0, OP.min, 7.0, OP.add)
+        ts(up, ind(v("lw"), v("offs", 32, 44)), col(LT4), OP.mult)
+        mmg(Z, picks(0, "up", 0, M))
+        mms(X, [(cmat(DU), v("rec")), (cmat(VALM), up)])
+        mm(Y, cmat(UPM), up, True, True)
+        ts(v("oi", 0, 12), Z, 0.5, OP.mult, 15.25, OP.add)
+        cp(new, v("oi", 0, 12))
+        act(flag, X, AF.Relu, -1.0)
+        act(stay, flag, AF.Identity, 1.0, -1.0)
+        act(tn, ind(v("tkw"), new), AF.Copy)
+        mm(X, cmat(ID), c1, True, True)
+        tt(tc, Y, flag, OP.mult)
+        tt(c1, X, stay, OP.mult)
+        ts(v("cu", lo, lo + M), c1, 15.0, OP.add)
+        mms(X, [spread(XT, lo, lo + M), (cmat(UT), tn)])
+        act(f1, X, AF.Abs)
+        act(v("qq"), f1, AF.Identity, 159.515625, 1.0 / 32)
+        nb = [spread(XK, lo, lo + M), (cmat(KK), tn), (cmat(ID64), v("qq"))]
+        mms(X, [(cmat(ID), v("mkc")), (fmat(ID32), f1)])
+        mms(Y, [(cmat(ID), v("mkc"))] + nb)
+        for x, o, c in ((X, 112, 1024.0), (Y, 80 + 16 * t, -1.0)):
+            scan(f2, v("d0"), x, BIG, OP.min, OP.max)
+            ts(v("offs", o, o + 12), v("bf", M + 15, 2 * M, 16), c, OP.add)
+        act(v("en", lo, lo + M), ind(v("rt"), v("offs", 112, 124)), AF.Copy)
+        if t == 0:
+            mms(X, [(cmat(NI), b1)] + nb)
+            tt(v("tb"), X, flag, OP.mult)
+
+    def products(t):
+        lo, a0 = (t % 2) * M, t * AW
+        if t >= 2:
+            pn = v("pn", lo, lo + M)
+            tt(pn, ind(v("aw", a0, a0 + AW), v("offs", 16 + 16 * t, 28 + 16 * t)), v("kg", C, C + M), OP.mult)
+            line("first")
+            mm(v("p0", 0, M), cmat(ONES), pn, True, True)
+            tt(v("wn"), v("p0", 0, M), v("flag", lo, lo + M), OP.mult)
+
+        def src(i0, i1):
+            if t == 0:
+                return ind(v("kw", SP, KWID), v("binu", i0, i1))
+            return ind(v("aw", a0, a0 + AW), v("cu", lo + i0, lo + i1))
+        hf, got, left, parts = 0, set(), list(SUMS), list(PARTS)
+        for (i0, i1), b in zip(PARTS, ("p1", "p2")):
+            mm(v(b, i0, i1), fmat(NON32), v("ub", t * M + i0, t * M + i1), True, False)
+        todo = [(i0, i1) for i0, i1, q in PIECES[min(t, 1)] if q == "s"]
+
+        def stage(b):
+            if todo:
+                i0, i1 = todo.pop(0)
+                mm(v("p%d" % (5 + b), 0, 16 * (i1 - i0)), cmat(NI), v("kg", 16 * i0, 16 * i1), True, True)
+                line("sums")
+        if t:
+            stage(0)
+            stage(1)
+        for i0, i1, q in PIECES[min(t, 1)]:
+            o, k = v("pr", t * C + 16 * i0, t * C + 16 * i1), v("kg", 16 * i0, 16 * i1)
+            if q == "v":
+                tt(o, src(i0, i1), k, OP.mult)
+                line("first")
+            else:
+                x = v("p%d" % (5 + hf), 0, 16 * (i1 - i0))
+                if t == 0:
+                    stage(hf)
+                act(v("ag", 16 * i0, 16 * i1), src(i0, i1), AF.Identity, 0.0, -1.0)
+                line("gather")
+                tt(o, x, v("ag", 16 * i0, 16 * i1), OP.mult)
+                line("first")
+                if t:
+                    stage(hf)
+                hf = 1 - hf
+            got.update(range(i0, i1))
+            for a, b in [x for x in left if got.issuperset(range(*x))]:
+                weights(t, "p0" if a < PARTS[0][1] else "p4", a, b)
+                line("sums")
+                left.remove((a, b))
+            while parts and not [x for x in left if x[0] < parts[0][1]]:
+                a, b = parts.pop(0)
+                elect(t, a, b, "p4" if a else "p0", "p2" if a else "p1")
 
     ratio_table()
     for c in range(3):
-        tk_gather("v", 0, 64 * c, 64 * c + 32)
-        tk_gather("s", 0, 64 * c + 32, 64 * c + 64)
-        tk_extract(0, 64 * c, 64 * c + 64)
-    bins(0)
+        tk_gather("v", 0, 64 * c, 64 * c + 36)
+        tk_gather("s", 0, 64 * c + 36, 64 * c + 64)
+        bins(0, 64 * c, 64 * c + 64, "p3", "p4")
+    for c in range(6):
+        act(v("kg", 512 * c, 512 * c + 512), ind(v("aw", 0, AW), v("cu", 32 * c, 32 * c + 32)), AF.Copy)
+        line("gather")
+    lags(0, "p4")
     steps(0)
-    for c in range(3):
-        act(v("kg", 1024 * c, 1024 * c + 1024), ind(v("aw", 0, W), v("cu", 64 * c, 64 * c + 64)), AF.Copy)
-    lags(0)
-    for a in range(RW, ZW, RW):
+    for a in [0] + list(range(PL, ZW, RW)) + [RW, 2 * RW]:
         b = min(a + RW, ZW)
-        dcopy("y", v("zb", a, b), v("zb", 0, b - a))
-        ops[-1]["r"] += v("binu", 0, M)[1]
+        dcopy("y", v("zb", a, b), v("zb", 3 * RW, 3 * RW + b - a))
+        ops[-1]["r"] += v("kg", 0, 16)[1]
 
     for t in range(R):
-        lo, a0, r0 = (t % 2) * M, t * W, t * RW
-        last, tag[0] = t == R - 1, str(t)
-        XA, XB = v("p2", 256, 384), v("p0", 448, 512)
-        mm(XA, v("ex32", p=(0, 8)), v("mbf", lo, lo + 128, p=(0, 8)), True, False)
-        for c in range(3):
-            a = t * C + 1024 * c
-            if t == 0:
-                tt(v("pr", a, a + 1024), ind(v("kw", 16, 2064), v("binu", 64 * c, 64 * c + 64)),
-                   v("kg", a, a + 1024), OP.mult)
-            elif c == 0:
-                tt(v("pr", a, a + 1024), ind(v("aw", a0, a0 + W), v("cu", lo, lo + 64)), v("kg", 0, 1024), OP.mult)
-            else:
-                for hf in range(2):
-                    b, i0 = 1024 * c + 512 * hf, lo + 64 * c + 32 * hf
-                    mm(v("p%d" % (5 + hf)), cmat(NI), v("kg", b, b + 512), True, True)
-                    act(v("ag", b - 1024, b - 512), ind(v("aw", a0, a0 + W), v("cu", i0, i0 + 32)), AF.Identity,
-                        0.0, -1.0)
-                    tt(v("pr", t * C + b, t * C + b + 512), v("p%d" % (5 + hf)), v("ag", b - 1024, b - 512), OP.mult)
-            for k in range(16):
-                mm(v("p0", 64 * c, 64 * c + 64) if c < 2 else v("p4", 0, 64), sel(k), v("pr", a + k, a + 1024, 16),
-                   k == 0, k == 15)
-        elect(t, 0, 128, v("p0", 0, 128), XA)
-        mm(XB, v("ex32", p=(0, 8)), v("mbf", lo + 128, lo + M, p=(0, 8)), True, False)
-        elect(t, 128, M, v("p4", 0, 64), XB)
-        if t == 0:
-            for c in range(3):
-                tk_gather("s", 1, 64 * c, 64 * c + 64)
-            ratio_fill()
-        for c in range(3):
-            ratios(t, c)
-        first_of(0, t % 2)
+        lo, a0, r0, last = (t % 2) * M, t * AW + 16, t * RW, t == R - 1
+        products(t)
+        first_of(t, 0)
         cp(ind(v("zb", r0, r0 + RW), v("offs", 0, 12)), v("oh", lo, lo + M))
-        send(2 + t, -1, "zb", r0 + 16 + E, "rv", t * GW, 1, 5, 2)
-        send(9 + t, -1, "zb", r0 + 16 + E, "rv", t * GW, 5, N, 2)
+        send(RAISES, -1, "zb", r0 + SP + E, "rv", t * GW)
         if t == 0:
-            tk_extract(1, 0, M)
+            for c in range(6):
+                tk_gather("s" if c < 4 else "v", 1, 32 * c, 32 * c + 32)
+                line("gather" if c < 4 else "planes")
+            bins(1, 0, M, "p3", "p2")
+            line("planes")
+            lags(1, "p2")
         if not last:
-            first_of(1, 2)
-            if t > 0:
-                steps(t + 1)
+            elected(t, 1, 0, M)
+            first_of(t, 1)
+            if t < 2:
+                candidates(t)
+            steps(t + 1)
             tt(v("kt"), ind(v("kw"), v("offs", 16, 28)), v("oh7", lo, lo + M), OP.min)
             tt(ind(v("kw"), v("offs", 16, 28)), v("kt"), v("oh", lo, lo + M), OP.add)
+            raise_k = len(ops) - 1
+        for c in range(3 if t < 2 else 0):
+            ratios(t, c)
         for hf in range(2):
             o = v("p%d" % (5 + hf))
             mm(o, cmat(NI if last else NSH), v("aw", a0 + 512 * hf, a0 + 512 * hf + 512), True, False)
-            mm(o, cmat(NI if last else NSH), v("zb", r0 + 16 + 512 * hf, r0 + 16 + 512 * hf + 512), False, False)
+            mm(o, cmat(NI if last else NSH), v("zb", r0 + SP + 512 * hf, r0 + SP + 512 * hf + 512), False, False)
         if not last:
-            if t == 0:
-                bins(1)
-                steps(1)
-                lags(1)
-            for c in range(3):
-                k_gather("s", t + 1, 64 * c, 64 * c + 64)
+            nx = M - lo
+            for c in range(0, M, 32):
+                act(v("kg", 16 * c, 16 * c + 512), ind(v("kw", SP, KWID), v("binu", nx + c, nx + c + 32)), AF.Copy)
+                line("gather")
+            if t:
+                act(v("kg", C, C + M), ind(v("kw", SP, KWID), v("offs", 64 + 16 * t, 76 + 16 * t)), AF.Copy)
         else:
             for c in range(3):
                 lam(t, c)
         for d in range(N - 1):
             pl = PL + d * E
             cp(ind(v("zb", pl, pl + E), v("snu", 8 * d, 8 * d + 8)), v("rv", t * GW + d * G, t * GW + (d + 1) * G))
+            line("planes")
+            if d == KPOS and not last:
+                ops[-1]["after"] = ops[-1]["after"] + [raise_k]
             for hf in range(2):
                 mm(v("p%d" % (5 + hf)), cmat(NUSH if last else NI), v("zb", pl + 512 * hf, pl + 512 * hf + 512),
                    False, d == N - 2)
@@ -688,19 +889,20 @@ def rank_program(g, core, T, topo):
                 o = v("yaf", 512 * hf, 512 * hf + 512)
                 ts(o, v("p%d" % (5 + hf)), -1.0, OP.mult, 15.0, OP.min)
                 store("y" if hf == 0 else "s", T.ya[:, 512 * hf:512 * hf + 512], o)
+                ops[-1]["end"] = True
             break
         ts(v("ash", 0, 512), v("p5"), 15.0, OP.add, 0.0, OP.max)
         act(v("ash", 512, E), v("p6"), AF.Relu, 15.0)
         f0 = (t + 2) * GW
-        ts(v("fb", f0, f0 + 448), ind(v("ash"), v("snu", 0, 28)), -1.0, OP.mult, 15.0, OP.add)
-        act(v("fb", f0 + 448, f0 + GW), ind(v("ash"), v("snu", 28, 56)), AF.Identity, 15.0, -1.0)
-        send(6 + t, 1, "fb", f0, "aw", a0 + W + E)
+        for d1, d2, _ in FORTH:
+            a, b = 8 * (d1 - 1), 8 * (d2 - 1)
+            c = (a + b) // 2
+            ts(v("fb", f0 + 16 * a, f0 + 16 * c), ind(v("ash"), v("snu", a, c)), -1.0, OP.mult, 15.0, OP.add)
+            act(v("fb", f0 + 16 * c, f0 + 16 * b), ind(v("ash"), v("snu", c, b)), AF.Identity, 15.0, -1.0)
+        send(FORTH, 1, "fb", f0, "aw", a0 + AW + E)
         for hf in range(2):
             mm(v("p%d" % (5 + hf)), cmat(NUSH), v("ash", 512 * hf, 512 * hf + 512), True, True)
-            act(v("aw", a0 + W + 512 * hf, a0 + W + 512 * hf + 512), v("p%d" % (5 + hf)), AF.Identity, 15.0)
-        if t < 2:
-            least(t)
-            candidates(t)
+            act(v("aw", a0 + AW + 512 * hf, a0 + AW + 512 * hf + 512), v("p%d" % (5 + hf)), AF.Identity, 15.0)
         for c in range(3):
             lam(t, c)
     emit(g, T, ops)

from concourse.bass import DstId, RemoteDMATransfer
from concourse.mybir import AluOpType as OP, ActivationFunctionType as AF

N, E, G, M, R = 8, 1024, 128, 192, 4
W = E + (N - 1) * G
GW = (N - 1) * G
C = 16 * M
SP = 208
RW = SP + W
PL = 4 * RW
ZW = PL + 7 * E
KWID = SP + 2048
AW = 16 + W
BIG = 4096.0
BF, F32, F16, I32, U16 = "bfloat16", "float32", "float16", "int32", "uint16"

(NI, NSH, NUSH, ID, ID64, EM, EL, ONES, NON, TRS, DM, DU, DLP, DLD, ELM, VALM, UPM, UT, KK, TRI) = range(20)
NON32, ID32, XBM = range(3)
XU0, XU1, XC, XT, XL0, XL1, XL2, XB, XK = range(9)
(P16, NXT, P12, P3, P1, KC8, K18, TCOL, NPAR, SGN, VALC, LT4, C15, NDZ, DCON, PQ, TB, MMUL, MADD, EAT,
 EBY) = range(21)

WHOLE = ((1, N, 1),)
RAISES = ((1, 3, 4), (3, 5, 4), (5, 7, 4), (7, N, 8))
FORTH = ((1, 5, 2), (5, N, 2))
PIECES = (((0, 32, "v"), (32, 64, "v"), (64, 96, "v"), (96, 128, "v"), (128, 160, "v"), (176, M, "s"), (160, 176, "v")),
          ((0, 64, "v"), (64, 96, "s"), (96, 128, "s"), (128, 160, "s"), (160, 180, "s"), (180, M, "s")))
SUMS = ((0, 64), (64, 128), (128, M))
PARTS = ((0, 128), (128, M))
LW = 512
KPOS = 3

SCRATCH = {}
for _n, _w, _d in (
        ("zb", ZW, BF), ("aw", R * AW, BF), ("ash", E, BF), ("tks", E, BF), ("tkw", AW, BF), ("fb", 5 * GW, BF),
        ("rv", R * GW, BF), ("kw", KWID, BF), ("kg", C + M, BF), ("tg", C, BF), ("ag", C, BF), ("pr", R * C, BF),
        ("rg", 2 * C, F32), ("so", 2048, F32), ("rt", 2048, F32), ("lw", E + 16, F32), ("yaf", E, F32),
        ("ylf", R * M, F32), ("e15", 2 * M, F32), ("t128", 128, I32), ("hl", 256, BF), ("dg", 256, BF),
        ("sni", 56, I32), ("snu", 56, U16), ("cai", 2 * M, I32), ("cu", 2 * M, U16), ("c1", 2 * M, F16),
        ("m8", 384, I32), ("m8h", 384, F16), ("mbf", 384, F32), ("ex", 8 * 128, BF), ("exv", 2 * 128, BF),
        ("bet", 8, F32), ("urep", R * M, BF), ("oh", 2 * M, BF), ("ji", 256, I32), ("pci", 8, I32),
        ("pcf", 24, F32), ("mk4", 8, F32), ("mc", 128, BF), ("cm", 20 * 128, BF), ("cf", 3 * 128, F32), ("w16", M, F16),
        ("ub", R * M, F32), ("pn", 2 * M, BF), ("en", 2 * M, F32), ("wn", M, F16), ("oi", 16, I32),
        ("sel", 32 * 128, BF), ("r16", M, BF), ("mkc", M, BF), ("d0", M, BF), ("big", M, BF), ("d12", 16, F32),
        ("w32", 2 * M, F32), ("wu", M, F32), ("hit", 2 * M, BF), ("hd", 3 * M, F16), ("rep", 2 * M, F16),
        ("lst", 3 * M, F32), ("zz", 12 * M, BF), ("sc", M, F32), ("offs", 136, U16), ("kt", M, BF),
        ("oh7", 2 * M, BF), ("ab", M, F32), ("qq", M, BF), ("bf", 2 * M, F32), ("b1", 2 * M, F16), ("l16", M, F16),
        ("binu", 2 * M, U16), ("up", M, F16), ("tn", M, BF), ("dlt", 2 * M, U16), ("rec", M, BF),
        ("flag", 3 * M, BF), ("tc", 2 * M, F16), ("tb", M, F16), ("ty", 4 * 120, F32), ("hi", 4 * 128, F32)):
    SCRATCH[_n] = ("sbuf", [128, _w], _d)
for _b in range(8):
    SCRATCH["p%d" % _b] = ("psum", [128, 512], F32)
NDMA = 44
NARR = 2 * len(WHOLE) + R * len(RAISES) + (R - 1) * len(FORTH)
SEMAPHORES = ["cv", "cs", "ct", "cg", "sent"] + ["arr%d" % _i for _i in range(NARR)] + ["dm%d" % _i for _i in range(NDMA)]

CY, PE, CALL, WAY, ROW, HOP = 0.00104, 0.00055, 0.5, 1.9, 0.0205, 0.1
CASES = ((0.8, 1.0, 1.0, 1.1, 0.1, 1.0, 1.0), (1.0, 1.15, 0.9, 1.2, 0.1, 1.2, 2.0), (1.15, 1.1, 1.45, 1.6, 0.15, 1.0, 2.5),
         (1.1, 1.33, 0.6, 0.9, 0.07, 1.0, 2.0), (1.0, 0.75, 1.3, 1.0, 0.1, 1.5, 1.0))
TRIES, STEPS, SLACK, PLAN = 5000, 600, 0.01, 1
ORDER = {}


def arrange(ops, pre):
    n = len(ops)
    queue = ["vstgyx".index(o["q"]) for o in ops]
    wait = [[(j, 0.0 if (ops[i]["q"] == "t" and ops[j]["q"] == "t") or j in ops[i].get("after", ()) else 1.0)
             for j in pre[i]] for i in range(n)]
    rank, stage, k = [0.0] * n, [n] * n, 0
    for i in range(n - 1, -1, -1):
        rank[i] += ops[i]["c"] + ops[i]["l"]
        for j, h in wait[i]:
            rank[j] = max(rank[j], rank[i] + (h * HOP if h else -ops[j]["l"]))
    for i in range(n):
        if ops[i]["k"] == "r" or ops[i].get("end"):
            k += 1
            todo = [i]
            while todo:
                j = todo.pop()
                if stage[j] == n:
                    stage[j] = k
                    todo.extend(pre[j])

    def place(key, case):
        cost, lag, ws, _ = case
        key = key[:]
        for i in range(n - 1, -1, -1):
            for j in pre[i]:
                if key[j] <= key[i]:
                    key[j] = key[i] + 1e-6
        start, done, rows = [0.0] * n, [0.0] * n, [([], []) for _ in range(5)]
        for i in sorted(range(n), key=lambda i: -key[i]):
            s, c = 0.0, cost[i]
            for j, h in ws[i]:
                if done[j] + h > s:
                    s = done[j] + h
            if queue[i] < 5:
                first, end = rows[queue[i]]
                lo, k = 0, len(end)
                while lo < k:
                    if end[(lo + k) // 2] > s:
                        k = (lo + k) // 2
                    else:
                        lo = (lo + k) // 2 + 1
                while k < len(end) and first[k] < s + c - 1e-9:
                    s = max(s, end[k])
                    k += 1
                first.insert(k, s)
                end.insert(k, s + c)
            start[i], done[i] = s, s + c + lag[i]
        return sorted(range(n), key=lambda i: (start[i], i)), key

    def waits(runs, step):
        _, i, by, _ = runs[step % len(runs)]
        pairs = []
        while by[i] >= 0:
            if by[i] not in pre[i]:
                pairs.append((by[i], i))
            i = by[i]
        return pairs

    def rerank(key):
        order, full = place(key, cases[PLAN])
        best, runs = worth(order)
        seed = 4321
        for step in range(TRIES):
            pairs = waits(runs, step)
            seed = (seed * 1103515245 + 12345) % 2147483648
            u, w = pairs[(seed >> 8) % len(pairs)]
            new, far = key[:], (seed >> 4) % 8 * 0.1 + 0.01
            if full[w] > full[u]:
                new[u] = key[u] + (1 if seed >> 20 & 1 else -1) * far * 4
            elif seed >> 20 & 1:
                new[w] = full[u] + far
            else:
                new[u] = full[w] - far
            o, f = place(new, cases[PLAN])
            end, r = worth(o)
            if end < best + SLACK:
                best, runs, order, key, full = end, r, o, new, f
        return order

    cases = []
    for f, ga, sc, tx, hop, pe, call in CASES:
        by = {"ga": f * ga, "sc": f * sc, "t": f * pe}
        cost = [o["c"] * by.get(o["m"] or o["q"], f) if o["k"] == "c" else o["c"] + (call - 1) * (0.1, CALL)[o["k"] == "r"]
                if o["k"] != "x" else 0.0 for o in ops]
        cases.append((cost, [o["l"] * (tx if o["k"] == "x" else 1.0) for o in ops],
                      [[(j, h * hop if h else -ops[j]["l"]) for j, h in w] for w in wait], f * (ga + sc + 2) + tx))

    def length(order, case, a=0, old=None):
        cost, lag, ws, _ = case
        done, by = (old[3][:], old[2][:]) if a else ([0.0] * n, [-1] * n)
        free, last, k = [0.0] * 6, [-1] * 6, a
        while k and -1 in last[:5]:
            k -= 1
            i = order[k]
            if queue[i] < 5 and last[queue[i]] < 0:
                free[queue[i]], last[queue[i]] = done[i] - lag[i], i
        for i in order[a:]:
            q = queue[i]
            s, b = free[q], last[q]
            for j, h in ws[i]:
                if done[j] + h > s:
                    s, b = done[j] + h, j
            by[i] = b
            s += cost[i]
            done[i] = s + lag[i]
            if q < 5:
                free[q], last[q] = s, i
        end = max(done)
        return end, done.index(end), by, done

    def worth(order, a=0, old=(None,) * 9):
        runs = [length(order, c, a, o) for c, o in zip(cases, old)]
        return sum(r[0] / c[3] for r, c in zip(runs, cases)), runs

    def refine(order):
        best, runs = worth(order)
        seed = 12345
        for step in range(STEPS):
            pairs = waits(runs, step)
            seed = (seed * 1103515245 + 12345) % 2147483648
            u, w = pairs[(seed >> 8) % len(pairs)]
            a, b = order.index(u), order.index(w)
            far = (seed >> 4) % 4
            if seed >> 20 & 1:
                while far and a > 0:
                    a -= 1
                    far -= queue[order[a]] == queue[w]
                part, need = order[a:b + 1], {w}
                for x in reversed(part):
                    if x in need:
                        need.update(pre[x])
                new = [x for x in part if x in need] + [x for x in part if x not in need]
            else:
                while far and b < n - 1:
                    b += 1
                    far -= queue[order[b]] == queue[w]
                part, need = order[a:b + 1], {u}
                for x in part:
                    if not need.isdisjoint(pre[x]):
                        need.add(x)
                new = [x for x in part if x not in need] + [x for x in part if x in need]
            if new == part:
                continue
            trial = order[:a] + new + order[b + 1:]
            end, r = worth(trial, a, runs)
            if end < best + SLACK * (1 - step / STEPS):
                best, runs, order = end, r, trial
        return order

    order = refine(rerank([rank[i] - 1000.0 * stage[i] for i in range(n)]))
    ORDER["end"] = [r[0] for r in worth(order)[1]]
    return order


def emit(g, T, ops):
    queues = {"v": g.vector, "s": g.scalar, "t": g.tensor, "g": g, "y": g.sync}
    log, bank, pre = {}, {}, []
    for i, o in enumerate(ops):
        d = set()
        for acc, wr in ((o["r"], False), (o["w"], True)):
            for (n, a, b) in acc:
                for (a2, b2, j, w2) in log.get(n, ()):
                    if a < b2 and a2 < b and (wr or w2):
                        d.add(j)
        for n in set(x[0] for x in o["r"] + o["w"]):
            if SCRATCH[n][0] == "psum":
                run = bank.setdefault(n, [o["q"], [], []])
                if run[0] != o["q"]:
                    run[0], run[1], run[2] = o["q"], [], run[1]
                d.update(run[2])
                if o["q"] == "t":
                    d.update(run[1][-1:])
                run[1].append(i)
        if o["k"] == "x":
            d.add(i - 1)
        pre.append(d)
        for (n, a, b) in o["w"]:
            log[n] = [x for x in log.get(n, []) if not (a <= x[0] and x[1] <= b)] + [(a, b, i, True)]
        for (n, a, b) in o["r"]:
            log.setdefault(n, []).append((a, b, i, False))
    key = len(ops)
    if key not in ORDER:
        ORDER[key] = arrange(ops, [d | set(o.get("after", ())) for d, o in zip(pre, ops)])
    order = ORDER[key]
    place = dict((i, p) for p, i in enumerate(order))
    deps = {}
    for i in order:
        o, best, keep = ops[i], {}, []
        for j in pre[i]:
            if o["k"] == "x" or (o["q"] == "t" and ops[j]["q"] == "t"):
                continue
            if ops[j]["k"] == "c":
                q = ops[j]["q"]
                if q not in best or place[j] > place[best[q]]:
                    best[q] = j
            else:
                assert ops[j]["k"] != "r"
                keep.append(j)
        deps[i] = sorted(keep + list(best.values()))
    needed = set(j for d in deps.values() for j in d)
    mark, total, waited, nd = {}, {}, {}, [0]
    for i in order:
        o = ops[i]
        if o["k"] == "x":
            mark[i] = (o["sem"], o["n"])
            total[o["sem"]] = o["n"]
            continue
        q = queues[o["q"]]
        for j in deps[i]:
            s, n = mark[j]
            if waited.get((o["q"], s), 0) < n:
                q.wait_ge(T.sem[s], n)
                waited[(o["q"], s)] = n
        ins = o["f"](q)
        if o["k"] == "d":
            s = "dm%d" % nd[0]
            nd[0] += 1
            ins.then_inc(T.sem[s], 16)
            mark[i] = (s, 16)
            total[s] = 16
        elif o["k"] == "r":
            total["sent"] = total.get("sent", 0) + o["n"]
        elif i in needed:
            s = "c" + o["q"]
            total[s] = total.get(s, 0) + 1
            ins.then_inc(T.sem[s], 1)
            mark[i] = (s, total[s])
    for s, n in total.items():
        if waited.get(("g", s), 0) < n:
            g.wait_ge(T.sem[s], n)


def rank_program(g, core, T, topo):
    rank = T.rank_of(core)
    if rank is None:
        return
    ops, sends, lines = [], [], {}

    def v(n, a=None, b=None, st=1, p=None):
        if a is None:
            a, b = 0, SCRATCH[n][1][1]
        ps = slice(0, 128) if p is None else slice(p[0], p[1])
        last = a + ((b - a - 1) // st) * st + 1
        ap = T[n][ps, a:b] if st == 1 else T[n][ps, a:last:st]
        return (ap, [(n, a, last)], (b - a - 1) // st + 1)

    def ind(w, o):
        return (w[0].indirect(o[0]), w[1] + o[1], 16 * o[2], w[1], o[1])

    def span(q, k, outs, ins, two):
        full = [x for x in outs + ins if isinstance(x, tuple)]
        wide = [SCRATCH[x[1][0][0]][2] in (F32, I32) for x in full if x[2] == full[0][2]]
        if k == "x":
            return 0.0, WAY
        if k == "r":
            return CALL, 0.0
        if k == "d":
            return 0.1, 2.0 + full[0][2] * (4 if wide[0] else 2) * 128 / 500e3
        n = outs[0][2]
        if q == "t":
            return max(64, n) * PE * (4 if SCRATCH[ins[1][1][0][0]][2] == F32 else 1), 0.0
        if q == "g":
            return 0.16 + 2 * n * CY, 0.0
        if len(outs[0]) == 5:
            return 0.06 + 3.8 * n * CY, 0.0
        if len(ins) and len(ins[0]) == 5:
            return 0.07 + 1.56 * n * CY, 0.0
        if q == "s":
            return 0.075 + n * CY, 0.0
        if two:
            return 0.06 + n * (1 if any(SCRATCH[x[1][0][0]][0] == "psum" for x in ins) else 2) * CY, 0.0
        return 0.06 + n * (1 if any(wide) else 0.5) * CY, 0.0

    def add(q, k, f, outs, ins, two=False, **kw):
        r, w = [], []
        for x in ins:
            if isinstance(x, tuple):
                r += x[1]
        for x in outs:
            if len(x) == 5:
                w += x[3]
                r += x[4]
            else:
                w += x[1]
        c, l = span(q, k, outs, ins, two)
        m = "sc" if outs and len(outs[0]) == 5 else "ga" if ins and len(ins[0]) == 5 else ""
        o = {"q": q, "k": k, "f": f, "r": r, "w": w, "c": c, "l": l, "m": m}
        o.update(kw)
        ops.append(o)

    def line(name):
        ops[-1]["after"] = lines.get(name, [])
        lines[name] = [len(ops) - 1]

    def ap(x):
        return x[0] if isinstance(x, tuple) else x

    def cp(o, i):
        add("v", "c", lambda e: e.tensor_copy(o[0], i[0]), [o], [i])

    def fill(o, c):
        add("v", "c", lambda e: e.memset(o[0], c), [o], [])

    def tt(o, a, b, op):
        add("v", "c", lambda e: e.tensor_tensor(o[0], a[0], b[0], op), [o], [a, b], True)

    def ts(o, a, s1, op0, s2=None, op1=None):
        if op1 is None:
            add("v", "c", lambda e: e.tensor_scalar(o[0], a[0], ap(s1), None, op0), [o], [a, s1])
        else:
            add("v", "c", lambda e: e.tensor_scalar(o[0], a[0], ap(s1), ap(s2), op0, op1), [o], [a, s1, s2])

    def scan(o, d0, d1, init, op0, op1):
        add("v", "c", lambda e: e.tensor_tensor_scan(o[0], d0[0], d1[0], ap(init), op0, op1), [o], [d0, d1, init])

    def vtr(o, i):
        add("v", "c", lambda e: e.transpose(o[0], i[0]), [o], [i])

    def recip(o, i):
        add("v", "c", lambda e: e.reciprocal(o[0], i[0]), [o], [i])

    def act(o, i, f, bias=0.0, scale=1.0):
        add("s", "c", lambda e: e.activation(o[0], i[0], f, bias=ap(bias), scale=ap(scale)), [o], [i, bias, scale])

    def move(q, o, i):
        if q == "v":
            cp(o, i)
        else:
            act(o, i, AF.Copy)

    def mm(o, l, r, start, stop):
        add("t", "c", lambda e: e.matmul(o[0], l[0], r[0], start, stop), [o], [l, r])

    def mms(o, pairs, start=True, stop=True):
        for j, (l, r) in enumerate(pairs):
            mm(o, l, r, start and j == 0, stop and j == len(pairs) - 1)

    def mmg(o, pairs, start=True, stop=True):
        def f(e):
            return [e.matmul(o[0], l[0], r[0], start and j == 0, stop and j == len(pairs) - 1)
                    for j, (l, r) in enumerate(pairs)][-1]
        add("t", "c", f, [o], [x for p in pairs for x in p])
        ops[-1]["c"] = sum(span("t", "c", [o], list(p), False)[0] for p in pairs)

    def iota(o, pat, base, ch, small=True):
        if small:
            add("g", "c", lambda e: e.iota(o[0], pat, base, ch, allow_small_or_imprecise_dtypes=True), [o], [])
        else:
            add("g", "c", lambda e: e.iota(o[0], pat, base, ch), [o], [])

    def gfill(o, c):
        iota(o, [[0, o[1][0][2] - o[1][0][1]]], c, 0)

    def asel(o, i, pat, base, ch, op, fl):
        add("g", "c", lambda e: e.affine_select(o[0], i[0], pat, op, fl, base, ch), [o], [i])

    def part(o, x):
        n, a, b = o[1][0]
        return (o[0], [(n, a + x, a + x + 1)], o[2])

    def load(q, o, src, x=None):
        o = o if x is None else part(o, x)
        add(q, "d", lambda e: e.dma_start(o[0], src), [o], [])
        line("load" + q)

    def store(q, dst, i):
        add(q, "d", lambda e: e.dma_start(dst, i[0]), [], [i])

    def dcopy(q, o, i):
        add(q, "d", lambda e: e.dma_start(o[0], i[0]), [o], [i])

    def send(calls, sign, sn, s0, dn, d0, ahead=0):
        for x, (d1, d2, k) in enumerate(calls):
            sem, tr, used = "arr%d" % len(sends), [], []
            for d in range(d1, d2):
                dst = T.cores[(rank + sign * d) % N]
                rid, pid = topo.addr(dst, core)
                en = [e for e in topo.engines(core, dst) if e not in used][:k]
                used += en
                tr.append(RemoteDMATransfer(
                    dst_ids=[DstId(rid=rid, pnc=pid)], dma_engine_mask=sum(1 << e for e in en), remote_sem=T.sem[sem],
                    src=T[sn][:, s0 + (d - 1) * G:s0 + d * G], dst=T[dn][:, d0 + (d - 1) * G:d0 + d * G]))
            n = (d2 - d1) * k
            add("g", "r", lambda e, tr=tr: e.remote_dma_fused(tr, local_sem=T.sem["sent"]), [],
                [v(sn, s0 + (d1 - 1) * G, s0 + (d2 - 1) * G)], n=n)
            line("send")
            if not sends:
                ops[-1]["c"] += 2.0
            sends.append(len(ops) - 1)
            add("x", "x", None, [v(dn, d0 + (d1 - 1) * G, d0 + (d2 - 1) * G)], [], sem=sem, n=n)
            ahead += 128 // k
            ops[-1]["l"] += ROW * ahead - CALL * x

    def cmat(i, p=None):
        return v("cm", i * 128, (i + 1) * 128, p=p)

    def fmat(i, p=None):
        return v("cf", i * 128, (i + 1) * 128, p=p)

    def sel(x):
        return v("sel", x * 128, (x + 1) * 128)

    def picks(s, n, a, b):
        return [(sel(s + k), v(n, a + k, b, 16)) for k in range(16)]

    def col(i, p=None):
        return v("pcf", i, i + 1, p=p)

    h, hb, hk = (0, 64), (32, 64), (64, 72)

    def spread(s, a, b):
        p, e = (hk, XB) if s == XK else (h, s)
        return (v("ex", e * 128, (e + 1) * 128, p=p), v("m8h", a, b, p=p))

    BET = v("bet", 0, 1)

    for x in range(2):
        load("y", v("t128", p=(64 * x, 64 * x + 32)), T.ti[:, 512 * x:512 * x + 512], x)
        load("s", v("t128", p=(64 * x + 32, 64 * x + 64)), T.kd[:, 512 * x:512 * x + 512], 2 + x)
    load("y", v("sni", p=(16, 128)), T.snd[0:112, :], 0)
    load("s", v("sni", p=(0, 16)), T.snd[112:128, :], 1)
    load("y", v("ash", p=(16, 128)), T.a0[0:112, :], 0)
    load("s", v("ash", p=(0, 16)), T.a0[112:128, :], 1)
    load("y", v("cai"), T.ca[:])
    load("s", BET, T.be[:])
    for s, src in ((XT, T.ti[:, 0:384]), (XK, T.kd[:, 0:384]), (XU0, T.us[:, 0:384]), (XU1, T.us[:, 384:768]),
                   (XC, T.cl[:]), (XL0, T.lp[:, 0:384]), (XL1, T.lp[:, 384:768]), (XL2, T.lp[:, 640:1024]),
                   (XB, T.bg[:])):
        load("y", v("m8", p=(8 * s, 8 * s + 8)), src, s)
    load("y", v("kw", SP, KWID), T.k0[:])
    load("y", v("aw", 16, 16 + E), T.a0[:])

    iota(v("pci", 0, 2), [[1, 2]], 0, 1, False)
    iota(v("ji", 0, 128), [[1, 128]], 512, -4, False)
    iota(v("mk4", 4, 8), [[4, 4]], 0, 0)
    iota(v("mc"), [[0, 8], [1, 16]], 0, 0)
    asel(v("mc"), v("mc"), [[-16, 8], [0, 16]], 0, 1, OP.is_ge, -2.0)
    asel(v("mc"), v("mc"), [[16, 8], [0, 16]], 15, -1, OP.is_ge, -2.0)
    iota(v("exv", 0, 128), [[-1, 8], [0, 16]], 0, 1)
    asel(v("exv", 128, 256), v("exv", 0, 128), [[0, 8], [1, 16]], -2, 0, OP.is_ge, -99.0)
    iota(v("r16"), [[0, 12], [1, 16]], 0, 0)
    iota(v("d12", 0, 12), [[-16, 12]], 176 - SP + 1, 0)

    ts(v("pci", 2, 4), v("pci", 0, 2), 15, OP.bitwise_and)
    for j, c in ((4, 12), (5, 3), (6, 1)):
        ts(v("pci", j, j + 1), v("pci", 0, 1), c, OP.bitwise_and)
    cp(v("pcf", 0, 5), v("pci", 2, 7))
    ts(v("ji", 128, 256), v("ji", 0, 128), 127, OP.bitwise_and)
    for c, a, b in ((EAT, 16.0, 18.0), (EBY, 1.0, 0.125)):
        fill(col(c), a)
        fill(col(c, (32, 64)), b)
        fill(col(c, (96, 128)), b)
    ts(cmat(EM), v("ji", 128, 256), col(EAT), OP.is_equal, col(EBY), OP.mult)
    ts(cmat(EL), v("ji", 128, 256), 17.0, OP.is_equal)
    ts(v("mk4", 0, 4), v("mk4", 4, 8), col(P12), OP.is_equal)
    ts(col(KC8), col(P3), 2.0, OP.is_equal, 8.0, OP.mult)
    act(col(K18), col(KC8), AF.Identity, 0.0, 1.0 / 64)

    cp(v("hl", 0, 128), v("t128"))
    cp(v("snu"), v("sni"))
    tt(v("hl", 128, 256), v("t128"), v("hl", 0, 128), OP.subtract)
    for x in range(2):
        a = (64 * x, 64 * x + 64)
        mms(v("p%d" % x, 0, 128), ((cmat(EM, a), v("hl", 0, 128, p=a)), (cmat(EL, a), v("hl", 128, 256, p=a))))
    ts(v("dg", 0, 128), v("p0", 0, 128), col(K18), OP.add)
    act(v("dg", 128, 256), v("p1", 0, 128), AF.Identity, col(K18))
    for x in range(8):
        o, i = v("tks", 128 * x, 128 * x + 128), v("dg", 128 * (x // 4), 128 * (x // 4) + 128)
        if x < 6:
            ts(o, i, v("mk4", x % 4, x % 4 + 1), OP.mult)
        else:
            act(o, i, AF.Identity, 0.0, v("mk4", x % 4, x % 4 + 1))
    act(v("fb", GW, 2 * GW), ind(v("ash"), v("snu")), AF.Copy)
    cp(v("fb", 0, 448), ind(v("tks"), v("snu", 0, 28)))
    act(v("fb", 448, GW), ind(v("tks"), v("snu", 28, 56)), AF.Copy)
    slots = [len(ops) - 2, len(ops) - 1]
    send(WHOLE, 1, "fb", 0, "tkw", 16 + E)
    send(WHOLE, 1, "fb", GW, "aw", 16 + E, 100)
    dcopy("y", v("tkw", 16, 16 + E, p=(0, 112)), v("tks", p=(16, 128)))
    ops[-1]["w"] = [("tkw", 17, 16 + E)]
    dcopy("y", part(v("tkw", 16, 16 + E, p=(112, 128)), 0), v("tks", p=(0, 16)))

    ts(v("cu"), v("cai"), 16.0, OP.add)
    ops[-1]["after"] = slots
    for x in range(16):
        ts(sel(x), v("mc"), float(x), OP.is_equal)
    fill(v("pcf", MMUL, MMUL + 2), 1.0)
    fill(col(MADD, (0, 32)), 0.0)
    fill(col(MMUL, (64, 128)), 8.0)
    fill(col(MADD, (64, 128)), -10240.0)
    ts(v("m8h", p=(0, 72)), v("m8", p=(0, 72)), col(MMUL, (0, 72)), OP.mult, col(MADD, (0, 72)), OP.add)
    ops[-1]["after"] = slots
    cp(v("mbf", p=hb), v("m8", p=hb))
    ops[-1]["after"] = slots
    for s in range(7):
        e0 = 128 if s >= XL0 else 0
        ts(v("ex", s * 128, (s + 1) * 128, p=h), v("exv", e0, e0 + 128, p=h), float(8 * s), OP.is_equal,
           -1.0 if s == XT else 1.0, OP.mult)
    ts(v("ex", XB * 128, (XB + 1) * 128, p=hk), v("exv", 0, 128, p=hk), 64.0, OP.is_equal)
    ts(fmat(XBM, hb), v("exv", 0, 128, p=hb), 56.0, OP.is_equal, 1.0 / 16, OP.mult)
    ts(v("c1"), v("cu"), -15.0, OP.add)
    ts(cmat(ONES), v("mc"), 0.0, OP.is_ge)
    ts(cmat(NON), v("mc"), 0.0, OP.is_ge, -1.0, OP.mult)
    act(fmat(NON32), cmat(NON), AF.Copy)
    ts(cmat(TRI), v("mc"), col(P16), OP.is_ge, 256.0, OP.mult)
    ts(col(TCOL), col(P3), 2.0, OP.is_lt)
    ts(col(LT4), col(P16), 4.0, OP.is_lt)
    ts(col(C15), col(P16), 15.0, OP.is_equal, -BIG, OP.mult)
    ts(col(NDZ), col(P16), 0.0, OP.not_equal, -1.0, OP.mult)
    act(col(NPAR), col(P1), AF.Identity, 0.0, -1.0)
    act(col(SGN), col(P1), AF.Identity, 1.0, -2.0)
    act(col(VALC), col(LT4), AF.Identity, 0.0, col(SGN))
    act(col(DCON), col(NDZ), AF.Identity, 0.0, -1024.0)
    act(col(PQ), col(P16), AF.Identity, 0.0, 1.0 / 16)
    act(col(TB), col(P16), AF.Identity, -128.0, -256.0)
    act(cmat(TRS), v("mc"), AF.Sigmoid, col(TB), 256.0)
    ops[-1]["c"] += 1.3
    ops[-1]["r"] += v("fb", 0, 2 * GW)[1]
    line("step")
    ts(cmat(ID), v("mc"), col(P16), OP.is_equal)
    for o, c in ((cmat(NI), -1.0), (cmat(ID64), 64.0), (fmat(ID32), 1.0), (cmat(DLD), col(NDZ))):
        act(o, cmat(ID), AF.Identity, 0.0, c)
    ts(cmat(DLP), v("mc"), col(NXT), OP.is_equal)
    ts(cmat(ELM), v("mc"), 2.0, OP.is_ge, col(C15), OP.mult)
    for i, c in ((VALM, VALC), (UT, TCOL), (KK, KC8)):
        act(cmat(i), cmat(ONES), AF.Identity, 0.0, col(c))
    act(cmat(UPM), cmat(VALM), AF.Relu)
    for x in range(16):
        if x < 8:
            asel(sel(16 + x), cmat(KK), [[0, 8], [1, 16]], -x, 0, OP.is_equal, 0.0)
            ops[-1]["after"] = sends[-1:]
        else:
            ts(sel(16 + x), v("mc"), float(x), OP.is_equal, col(KC8), OP.mult)
    for b, s in (("p5", XU0), ("p6", XU1), ("p4", XC)):
        mms(v(b, 0, 384), (spread(s, 0, 384),))
    act(v("urep", 0, 384), v("p5", 0, 384), AF.Copy)
    act(v("urep", 384, 768), v("p6", 0, 384), AF.Copy)
    ts(v("oh"), v("p4", 0, 384), col(P16), OP.is_equal)
    mms(v("p7", 0, 384), ((fmat(XBM, hb), v("mbf", p=hb)),))
    for x in range(2):
        tt(v("ub", 384 * x, 384 * x + 384), v("p7", 0, 384), v("urep", 384 * x, 384 * x + 384), OP.mult)
    act(v("oh7"), v("oh"), AF.Identity, 7.0, -1.0)
    ts(v("mkc"), v("r16"), col(P16), OP.not_equal, -BIG, OP.mult)
    ts(v("big"), v("r16"), 0.0, OP.is_equal, 1.0e6, OP.mult)
    gfill(v("d0"), int(BIG))
    ts(v("d0", 0, M, 16), v("d12", 0, 12), col(P16), OP.add)
    row = [[-1, 128]]
    iota(v("ty", 0, 17), [[1, 17]], 0, 0)
    for o, c in [(v("ty", 120, 239), 0), (v("ty", 240, 359), 1), (v("hi", 0, 128), 0), (v("tkw", 0, 16), 0),
                 (v("aw", 0, 16), 0), (v("kw", 0, SP), 0)]:
        gfill(o, c)
    for i, op, b in ((DM, OP.is_equal, -1), (DU, OP.is_gt, 0)):
        asel(cmat(i), cmat(NON), row, b, 1, op, 0.0)
        ops[-1]["after"] = sends[-1:]
        asel(cmat(i), cmat(i), row, 0, 1, OP.not_equal, 1.0)
    for o in ([v("zb", a, a + 532) for a in range(3 * RW, PL, 532)] + [v("aw", t * AW, t * AW + 16) for t in range(1, R)]
              + [v("lw", 0, 8), v("lw", E + 8, E + 16), v("cm", NSH * 128, (NUSH + 1) * 128)]):
        gfill(o, 0)
    for i, bases in ((NSH, (16, -112)), (NUSH, (-16, 112))):
        for b in bases:
            asel(cmat(i), cmat(i), row, b, 1, OP.not_equal, -1.0)
    for p, s, a, b, c in (("p5", XL0, 0, 384, 8), ("p6", XL1, 0, 384, 392), ("p3", XL2, 128, 384, 776)):
        mms(v(p, 0, b - a), (spread(s, a, b),))
        act(v("lw", c, c + b - a), v(p, 0, b - a), AF.Relu, col(NPAR))

    def ratio_table():
        for n in range(1, 7):
            ts(v("ty", 120 + n, 239, 7), v("ty", 0, 17), BET, OP.mult, -1.0 / (7 - n), OP.mult)
            ops[-1]["w"] = [("ty", 120 + n, 121 + n)]
            ops[-1]["after"] = slots
        scan(v("ty", 360, 479), v("ty", 120, 239), v("ty", 240, 359), 0.0, OP.mult, OP.add)
        ts(v("hi", 128, 256), v("hi", 0, 128), v("ty", 478, 479), OP.add)
        scan(v("hi", 256, 321), v("hi", 128, 193), v("hi", 0, 65), 1.0, OP.mult, OP.add)
        recip(v("hi", 336, 337), v("hi", 320, 321))
        scan(v("hi", 384, 512), v("hi", 128, 256), v("hi", 0, 128), v("hi", 336, 337), OP.mult, OP.add)
        for b in range(16):
            act(v("rt", b, 2048, 16), v("hi", 384, 512), AF.Identity, 0.0, v("ty", 366 + 7 * b, 367 + 7 * b))
            ops[-1]["w"] = [("rt", b, b + 1)]
            line("step")

    def tk_gather(q, t, i0, i1):
        move(q, v("tg", 16 * i0, 16 * i1), ind(v("tkw"), v("cu", t * M + i0, t * M + i1)))

    def bins(t, i0, i1, bx, by):
        lo = t * M
        X, Y, a, q = v(bx, i0, i1), v(by, M + i0, M + i1), v("ab", i0, i1), v("qq", i0, i1)
        for c in range(i0, i1, 64):
            mmg(v(bx, c, c + 64), [spread(XT, lo + c, lo + c + 64)] + picks(0, "tg", 16 * c, 16 * c + 1024))
        act(a, X, AF.Abs, -0.5625)
        act(q, a, AF.Identity, 159.515625, 1.0 / 32)
        mm(Y, *spread(XK, lo + i0, lo + i1), True, False)
        for c in range(i0, i1, 64):
            mmg(v(by, M + c, M + c + 64), picks(16, "tg", 16 * c, 16 * c + 1024), False, False)
        mm(Y, cmat(ID64), q, False, True)
        ts(v("binu", lo + i0, lo + i1), Y, -1.0, OP.add)

    def lags(t, by):
        cp(v("b1", t * M, (t + 1) * M), v(by, M, 2 * M))
        ts(v("l16"), v("ab"), 1024.0, OP.add)
        mms(v("p3", 0, M), [(cmat(i), v("l16")) for i in (DLP, DLD)])
        ts(v("dlt", t * M, (t + 1) * M), v("p3", 0, M), col(DCON), OP.add)

    def steps(t):
        lo = (t % 2) * M
        mms(v("p7", 0, M), [(cmat(DM), v(n, lo, lo + M)) for n in (("c1",) if t < 2 else ("c1", "tc"))])
        if t < R - 1:
            mms(v("p7", M, 2 * M), [(cmat(DM), v("b1", lo, lo + M))] + [(cmat(DM), v("tb"))] * (t // 2))

    def elected(t, j, i0, i1):
        s = 2 if j else t % 2
        a, b = s * M + i0, s * M + i1
        tt(v("hd", a, b), v("p7", j * M + i0, j * M + i1), v("hit", (t % 2) * M + i0, (t % 2) * M + i1), OP.mult)
        mm(v("p0", i0, i1), cmat(ONES), v("hd", a, b), True, True)
        cp(v("rep", j * M + i0, j * M + i1), v("p0", i0, i1))
        li = v("p1" if i0 == 0 else "p2", 256 + i0, 256 + i1)
        mms(li, [(cmat(ID), v("mkc", i0, i1)), (cmat(ONES), v("hd", a, b))])
        scan(v("lst", a, b), v("d0", i0, i1), li, BIG, OP.min, OP.max)

    def weights(t, bank, i0, i1):
        mmg(v(bank, 256 + i0, 256 + i1), picks(0, "pr", t * C + 16 * i0, t * C + 16 * i1)
            + [(cmat(ID), v("wn", i0, i1))] * (t // 2))

    def elect(t, i0, i1, wb, db):
        lo = (t % 2) * M
        w, w32, wu, D = v(wb, 256 + i0, 256 + i1), v("w32", lo + i0, lo + i1), v("wu", i0, i1), v(db, i0, i1)
        tt(wu, w, v("urep", t * M + i0, t * M + i1), OP.mult)
        cp(v("w16", i0, i1), w)
        mms(D, [(cmat(TRI), v("w16", i0, i1)), (fmat(NON32), wu)], False)
        if t < 2:
            act(w32, w, AF.Identity, col(PQ))
        act(v("hit", lo + i0, lo + i1), D, AF.Sigmoid, -128.0, 256.0)
        line("step")
        elected(t, 0, i0, i1)

    def first_of(t, j):
        s = 2 if j else t % 2
        mms(v("p4", 0, M), [(cmat(ID), v("mkc")), (cmat(ONES), v("hd", s * M, (s + 1) * M))], True, False)
        for y in range(12):
            z0, z1 = y * M + 16 * y, (y + 1) * M
            ts(v("zz", z0, z1), v("rep", j * M + 16 * y, (j + 1) * M),
               v("lst", s * M + 16 * y + 15, s * M + 16 * y + 16), OP.is_equal, -BIG, OP.mult)
            if y < 11:
                mm(v("p4", 16 * y + 16, M), cmat(ONES), v("zz", z0 + 16, z1), False, False)
            mm(v("p4", 16 * y, 16 * y + 16), cmat(TRS), v("zz", z0, z0 + 16), False, y == 11)
        scan(v("sc"), v("d0"), v("p4", 0, M), BIG, OP.min, OP.max)
        ts(v("offs", 16 * j, 16 * j + 12), v("sc", 15, M, 16), SP - 1.0, OP.add)

    def ratios(t, c):
        a, e = t * C + 1024 * c, t * M + 64 * c
        for b in range(2):
            act(v("rg", a + 512 * b, a + 512 * b + 512), ind(v("rt"), v("dlt", e + 32 * b, e + 32 * b + 32)), AF.Copy)
        act(v("e15", e, e + 64), v("rg", a, a + 1024, 16), AF.Copy)
        act(v("rg", a, a + 1024, 16), v("e15", e, e + 64), AF.Identity, 0.0, 0.0)

    def lam(t, c):
        a, so = 1024 * c, 1024 * ((3 * t + c) % 2)
        lo, y = (t % 2) * M, v("ylf", t * M, (t + 1) * M)
        for b in range(0, 1024, LW):
            scan(v("so", so + b, so + b + LW), v("rg", 16 * lo + a + b, 16 * lo + a + b + LW),
                 v("pr", t * C + a + b, t * C + a + b + LW), 0.0, OP.mult, OP.add)
        tt(v("ylf", t * M + 64 * c, t * M + 64 * c + 64), v("so", so + 15, so + 1024, 16),
           v("e15", lo + 64 * c, lo + 64 * c + 64), OP.mult)
        if c == 2:
            if t >= 2:
                new = v("en", lo, lo + M)
                tt(new, new, v("pn", lo, lo + M), OP.mult)
                tt(y, y, new, OP.add)
            store("y", T.yl[:, t * M:(t + 1) * M], y)

    def candidates(t):
        lo = t * M
        X, Y, Z = v("p3", 0, M), v("p3", M, 2 * M), v("p3", 400, 412)
        up, stay, tn = v("up"), v("flag", 2 * M, 3 * M), v("tn")
        c1, b1, tc, flag = [v(n, lo, lo + M) for n in ("c1", "b1", "tc", "flag")]
        new = v("offs", 48 + 16 * t, 60 + 16 * t)
        f1, f2 = [v("bf", j * M, (j + 1) * M) for j in range(2)]
        vtr(f1, v("w32", lo, lo + M))
        scan(f2, v("big"), f1, 0.0, OP.add, OP.min)
        vtr(X, f2)
        tt(v("rec"), v("w32", lo, lo + M), X, OP.is_equal)
        mms(Y, [spread(XL0, lo, lo + M), (cmat(ELM), v("hit", lo, lo + M)), (cmat(ONES), v("hd", lo, lo + M))])
        act(v("lw", 8 + lo, 8 + lo + M), Y, AF.Relu, col(NPAR))
        ts(v("offs", 32, 44), v("lst", lo + 15, lo + M, 16), 1025.0, OP.min, 7.0, OP.add)
        ts(up, ind(v("lw"), v("offs", 32, 44)), col(LT4), OP.mult)
        mmg(Z, picks(0, "up", 0, M))
        mms(X, [(cmat(DU), v("rec")), (cmat(VALM), up)])
        mm(Y, cmat(UPM), up, True, True)
        ts(v("oi", 0, 12), Z, 0.5, OP.mult, 15.25, OP.add)
        cp(new, v("oi", 0, 12))
        act(flag, X, AF.Relu, -1.0)
        act(stay, flag, AF.Identity, 1.0, -1.0)
        act(tn, ind(v("tkw"), new), AF.Copy)
        mm(X, cmat(ID), c1, True, True)
        tt(tc, Y, flag, OP.mult)
        tt(c1, X, stay, OP.mult)
        ts(v("cu", lo, lo + M), c1, 15.0, OP.add)
        mms(X, [spread(XT, lo, lo + M), (cmat(UT), tn)])
        act(f1, X, AF.Abs)
        act(v("qq"), f1, AF.Identity, 159.515625, 1.0 / 32)
        nb = [spread(XK, lo, lo + M), (cmat(KK), tn), (cmat(ID64), v("qq"))]
        mms(X, [(cmat(ID), v("mkc")), (fmat(ID32), f1)])
        mms(Y, [(cmat(ID), v("mkc"))] + nb)
        for x, o, c in ((X, 112, 1024.0), (Y, 80 + 16 * t, -1.0)):
            scan(f2, v("d0"), x, BIG, OP.min, OP.max)
            ts(v("offs", o, o + 12), v("bf", M + 15, 2 * M, 16), c, OP.add)
        act(v("en", lo, lo + M), ind(v("rt"), v("offs", 112, 124)), AF.Copy)
        if t == 0:
            mms(X, [(cmat(NI), b1)] + nb)
            tt(v("tb"), X, flag, OP.mult)

    def products(t):
        lo, a0 = (t % 2) * M, t * AW
        if t >= 2:
            pn = v("pn", lo, lo + M)
            tt(pn, ind(v("aw", a0, a0 + AW), v("offs", 16 + 16 * t, 28 + 16 * t)), v("kg", C, C + M), OP.mult)
            line("first")
            mm(v("p0", 0, M), cmat(ONES), pn, True, True)
            tt(v("wn"), v("p0", 0, M), v("flag", lo, lo + M), OP.mult)

        def src(i0, i1):
            if t == 0:
                return ind(v("kw", SP, KWID), v("binu", i0, i1))
            return ind(v("aw", a0, a0 + AW), v("cu", lo + i0, lo + i1))
        hf, got, left, parts = 0, set(), list(SUMS), list(PARTS)
        for (i0, i1), b in zip(PARTS, ("p1", "p2")):
            mm(v(b, i0, i1), fmat(NON32), v("ub", t * M + i0, t * M + i1), True, False)
        todo = [(i0, i1) for i0, i1, q in PIECES[min(t, 1)] if q == "s"]

        def stage(b):
            if todo:
                i0, i1 = todo.pop(0)
                mm(v("p%d" % (5 + b), 0, 16 * (i1 - i0)), cmat(NI), v("kg", 16 * i0, 16 * i1), True, True)
                line("sums")
        if t:
            stage(0)
            stage(1)
        for i0, i1, q in PIECES[min(t, 1)]:
            o, k = v("pr", t * C + 16 * i0, t * C + 16 * i1), v("kg", 16 * i0, 16 * i1)
            if q == "v":
                tt(o, src(i0, i1), k, OP.mult)
                line("first")
            else:
                x = v("p%d" % (5 + hf), 0, 16 * (i1 - i0))
                if t == 0:
                    stage(hf)
                act(v("ag", 16 * i0, 16 * i1), src(i0, i1), AF.Identity, 0.0, -1.0)
                line("gather")
                tt(o, x, v("ag", 16 * i0, 16 * i1), OP.mult)
                line("first")
                if t:
                    stage(hf)
                hf = 1 - hf
            got.update(range(i0, i1))
            for a, b in [x for x in left if got.issuperset(range(*x))]:
                weights(t, "p0" if a < PARTS[0][1] else "p4", a, b)
                line("sums")
                left.remove((a, b))
            while parts and not [x for x in left if x[0] < parts[0][1]]:
                a, b = parts.pop(0)
                elect(t, a, b, "p4" if a else "p0", "p2" if a else "p1")

    ratio_table()
    for c in range(3):
        tk_gather("v", 0, 64 * c, 64 * c + 36)
        tk_gather("s", 0, 64 * c + 36, 64 * c + 64)
        bins(0, 64 * c, 64 * c + 64, "p3", "p4")
    for c in range(6):
        act(v("kg", 512 * c, 512 * c + 512), ind(v("aw", 0, AW), v("cu", 32 * c, 32 * c + 32)), AF.Copy)
        line("gather")
    lags(0, "p4")
    steps(0)
    for a in [0] + list(range(PL, ZW, RW)) + [RW, 2 * RW]:
        b = min(a + RW, ZW)
        dcopy("y", v("zb", a, b), v("zb", 3 * RW, 3 * RW + b - a))
        ops[-1]["r"] += v("kg", 0, 16)[1]

    for t in range(R):
        lo, a0, r0, last = (t % 2) * M, t * AW + 16, t * RW, t == R - 1
        products(t)
        first_of(t, 0)
        cp(ind(v("zb", r0, r0 + RW), v("offs", 0, 12)), v("oh", lo, lo + M))
        send(RAISES, -1, "zb", r0 + SP + E, "rv", t * GW)
        if t == 0:
            for c in range(6):
                tk_gather("s" if c < 4 else "v", 1, 32 * c, 32 * c + 32)
                line("gather" if c < 4 else "planes")
            bins(1, 0, M, "p3", "p2")
            line("planes")
            lags(1, "p2")
        if not last:
            elected(t, 1, 0, M)
            first_of(t, 1)
            if t < 2:
                candidates(t)
            steps(t + 1)
            tt(v("kt"), ind(v("kw"), v("offs", 16, 28)), v("oh7", lo, lo + M), OP.min)
            tt(ind(v("kw"), v("offs", 16, 28)), v("kt"), v("oh", lo, lo + M), OP.add)
            raise_k = len(ops) - 1
        for c in range(3 if t < 2 else 0):
            ratios(t, c)
        for hf in range(2):
            o = v("p%d" % (5 + hf))
            mm(o, cmat(NI if last else NSH), v("aw", a0 + 512 * hf, a0 + 512 * hf + 512), True, False)
            mm(o, cmat(NI if last else NSH), v("zb", r0 + SP + 512 * hf, r0 + SP + 512 * hf + 512), False, False)
        if not last:
            nx = M - lo
            for c in range(0, M, 32):
                act(v("kg", 16 * c, 16 * c + 512), ind(v("kw", SP, KWID), v("binu", nx + c, nx + c + 32)), AF.Copy)
                line("gather")
            if t:
                act(v("kg", C, C + M), ind(v("kw", SP, KWID), v("offs", 64 + 16 * t, 76 + 16 * t)), AF.Copy)
        else:
            for c in range(3):
                lam(t, c)
        for d in range(N - 1):
            pl = PL + d * E
            cp(ind(v("zb", pl, pl + E), v("snu", 8 * d, 8 * d + 8)), v("rv", t * GW + d * G, t * GW + (d + 1) * G))
            line("planes")
            if d == KPOS and not last:
                ops[-1]["after"] = ops[-1]["after"] + [raise_k]
            for hf in range(2):
                mm(v("p%d" % (5 + hf)), cmat(NUSH if last else NI), v("zb", pl + 512 * hf, pl + 512 * hf + 512),
                   False, d == N - 2)
        if last:
            for hf in range(2):
                o = v("yaf", 512 * hf, 512 * hf + 512)
                ts(o, v("p%d" % (5 + hf)), -1.0, OP.mult, 15.0, OP.min)
                store("y" if hf == 0 else "s", T.ya[:, 512 * hf:512 * hf + 512], o)
                ops[-1]["end"] = True
            break
        ts(v("ash", 0, 512), v("p5"), 15.0, OP.add, 0.0, OP.max)
        act(v("ash", 512, E), v("p6"), AF.Relu, 15.0)
        f0 = (t + 2) * GW
        for d1, d2, _ in FORTH:
            a, b = 8 * (d1 - 1), 8 * (d2 - 1)
            c = (a + b) // 2
            ts(v("fb", f0 + 16 * a, f0 + 16 * c), ind(v("ash"), v("snu", a, c)), -1.0, OP.mult, 15.0, OP.add)
            act(v("fb", f0 + 16 * c, f0 + 16 * b), ind(v("ash"), v("snu", c, b)), AF.Identity, 15.0, -1.0)
        send(FORTH, 1, "fb", f0, "aw", a0 + AW + E)
        for hf in range(2):
            mm(v("p%d" % (5 + hf)), cmat(NUSH), v("ash", 512 * hf, 512 * hf + 512), True, True)
            act(v("aw", a0 + AW + 512 * hf, a0 + AW + 512 * hf + 512), v("p%d" % (5 + hf)), AF.Identity, 15.0)
        for c in range(3):
            lam(t, c)
    emit(g, T, ops)
